import numpy as np, ml_dtypes
CORES = [10,34,74,98]
N = 4
import mx_ref
BF = ml_dtypes.bfloat16
def gentries(a):
    return np.ascontiguousarray(a.reshape(8, 16, -1).transpose(0, 2, 1)).reshape(8, -1)
def gtable(e):
    e = np.asarray(e); return np.ascontiguousarray(e.reshape(8, -1, 16).transpose(0, 2, 1)).reshape(128, -1).astype(np.int32)
def gcols(t, e):
    v = np.concatenate([t.reshape(8, 16, -1, 4), np.zeros((8, 16, 1, 4), BF)], axis=2)
    return np.ascontiguousarray(np.stack([v[g][:, e[g]] for g in range(8)])).reshape(128, -1)
def tile(rs):
    return np.stack(rs, axis=2).reshape(128, -1).astype(BF)
def pick(q, e):
    c = np.concatenate([q[0].reshape(128, -1, 4), np.zeros((128, 1, 4), np.uint8)], axis=1); s = np.concatenate([q[1], np.ones((16, 1), np.uint8)], axis=1)
    return (np.ascontiguousarray(c[:, e].reshape(128, -1)), np.ascontiguousarray(s[:, e]))
def join(*qs):
    return (np.concatenate([q[0] for q in qs], axis=1), np.concatenate([q[1] for q in qs], axis=1))
def put(q, e, v):
    c, s = q[0].reshape(128, -1, 4).copy(), q[1].copy(); c[:, e] = v[0].reshape(128, -1, 4); s[:, e] = v[1]
    return (c.reshape(128, -1), s)
def pk(c, s):
    return (np.ascontiguousarray(c), mx_ref.live(s))
def emit(q):
    return q[0], q[1]
def packed(v, rng):
    q = [mx_ref.quantize(np.ascontiguousarray(v[r])) for r in range(N)]
    return np.stack([a for a, b in q]), np.stack([mx_ref.plane(b, rng) for a, b in q])
def values_of_codes():
    e, c = np.zeros((128, 128, 4), np.float32), np.zeros((128, 2, 4), np.uint8)
    e[np.arange(128), np.arange(128), 0] = 1
    c[:127, :, 0] = np.arange(256).reshape(2, 128).T[:127]
    return mx_ref.matmul(mx_ref.quantize(e.reshape(128, 512).astype(BF)), (c.reshape(128, 8), np.full((16, 2), 127, np.uint8))).T.reshape(-1).astype(np.float64)
CODE_VALUE, SCALE_VALUE = values_of_codes(), 2.0 ** (np.arange(256) - 127.0)
def decode(q):
    return (CODE_VALUE[q[0]].reshape(16, 8, -1, 4) * SCALE_VALUE[q[1]][:, None, :, None] + 0.0).reshape(128, -1).astype(np.float32)
def f(rng, *shape):
    return mx_ref.flush((rng.standard_normal(shape, dtype=np.float32) * np.exp2(rng.integers(-2, 3, shape[:-1] + (1,)))).astype(BF))
def wide(rng, *shape, cols=0):
    v = rng.standard_normal(shape, dtype=np.float32) * np.exp2(rng.integers(-12, 13, shape)).astype(np.float32)
    if cols: v *= np.repeat(np.exp2(rng.integers(-cols, cols + 1, shape[:-2] + (1, shape[-1] // 4))) * (rng.random(shape[:-2] + (1, shape[-1] // 4)) > 0.0625), 4, axis=-1).astype(np.float32)
    return mx_ref.flush(v.astype(BF))
C = 448
STEP = [1, 2, 3]
def big(v):
    v = v.astype(np.float32)
    v[np.abs(v) < np.float32(2.0 ** -16)] = 0
    return v.astype(BF)
def numbers_of(rng):
    return {"x": big(f(rng, N, 128, 4 * C)), "u": np.array(f(rng, N, 128, 512)), "v": np.array(f(rng, N, 128, 512))}
def stored(k, t):
    return {"gl": np.stack([gtable(k[r]) for r in range(N)]), "ht": np.stack([gtable(t[r]) for r in range(N)])}
def lists(rng):
    e = np.tile(np.arange(C), (N, 8, 1))
    k = np.stack([rng.permuted(e, axis=2), rng.permuted(e, axis=2)], axis=3).reshape(N, 8, 2 * C)
    return stored(k, rng.integers(0, C, (N, 8, C)))
def layers(rng):
    return big(f(rng, N, 128, 2048)).reshape(N, 8, 16, 4, 8, 16, 4)
def weights(rng, w):
    c, p = packed(np.ascontiguousarray(w).reshape(N, 128, 2048), rng)
    return {"wc": c, "ws": p}
def setup_inputs(rng):
    return {**numbers_of(rng), **lists(rng), **weights(rng, layers(rng))}
def setup_inputs_ties(rng):
    d = numbers_of(rng)
    o = rng.permutation(N)
    k = rng.integers(-1, 2, (N, 8, C)).astype(np.float32)
    k[o[1]] = 1
    x = d["x"].reshape(N, 8, 16, C, 4)
    x[:, :, 0] = 0
    x[:, :, 0, :, 0] = k.astype(BF)
    c = np.ones(N, np.float32)
    c[o[0]] = 0
    c[o[2]] = -1
    u = d["u"].reshape(N, 128, 128, 4)
    u[:, :, ::16] = 0
    for h in range(0, 128, 16): u[:, h, h, 0] = c.astype(BF)
    w = layers(rng)
    w[:, :, :, :, :, :8] = 0
    return {"x": x.reshape(N, 128, 4 * C), "u": u.reshape(N, 128, 512), "v": d["v"], **lists(rng), **weights(rng, w)}
def setup_inputs_near(rng):
    d = numbers_of(rng)
    o = rng.permutation(N) % 2
    k = np.where(o == 0, 2.0 ** -30, 1.0).astype(np.float32)
    x = np.zeros((N, 8, 16, C, 4), np.float32)
    s = rng.integers(-1, 2, (N, 8, C)) * k[:, None, None]
    x[:, :, 0, :, 0] = 1.125 * s
    x[:, :, 1, :, 0] = -1.25 * s
    for r in range(N):
        for g in rng.permutation(8)[:4]: x[r, g, 0, rng.integers(C), 0] = 2.0 ** 30 * rng.choice([-1.0, 1.0])
    i = np.arange(N)
    e = ((i ^ (i >> 1) ^ (i >> 2))[:, None] + rng.permutation(8)) % 2
    a = (1 + (2 * rng.integers(0, 64, (N, 8, 8, C, 4)) + 1) * 2.0 ** -7) * np.exp2(12.0 - rng.integers(8, 15, (N, 8, 8, C, 4)))
    a[:, :, 0, :, 0] = -1.96875 * 2.0 ** 12
    a = np.where(e[:, :, None, None, None] == 0, -2.0 ** 26, a)
    x[:, :, 8:] = np.where(rng.random((N, 8, 1, C, 1)) < 0.5, a, 0.0)
    u = d["u"].reshape(N, 128, 128, 4)
    u[:, :, ::16] = 0
    for h in range(0, 128, 16):
        u[:, h, h, 0] = (1.125 * k).astype(BF)
        u[:, h + 1, h, 0] = k.astype(BF)
    w = layers(rng)
    w[:, :, :8] = 0
    w[:, :, :, :, :, :8] = 0
    return {"x": x.reshape(N, 128, 4 * C).astype(BF), "u": u.reshape(N, 128, 512), "v": d["v"], **lists(rng), **weights(rng, w)}
def setup_inputs_late(rng):
    d = numbers_of(rng)
    c = (rng.permutation(N) % 2 * 2.0 - 1.0).astype(np.float32).astype(BF)
    x = d["x"].reshape(N, 8, 16, C, 4)
    x[:, :, 0] = c[:, None, None, None]
    u = d["u"].reshape(N, 128, 128, 4)
    u[:, :, ::16] = 0
    for h in range(0, 128, 16): u[:, h, h, 0] = 1
    w = layers(rng)
    w[:, :, :, :, :, 0] = (w[:, :, :, :, :, 0].astype(np.float32) * 4).astype(BF)
    return {"x": x.reshape(N, 128, 4 * C), "u": u.reshape(N, 128, 512), "v": d["v"], **lists(rng), **weights(rng, w)}
def setup_inputs_ends(rng):
    d = numbers_of(rng)
    o, e = rng.permutation(N) % 4, rng.permutation(N) % 4
    s = rng.choice([-1.0, 1.0], (N, 128, C, 4))
    s[o == 0] = -1
    s[o == 1] = rng.choice([-1.0, 1.0], (N, 1, C, 1))[o == 1]
    x = s * (0.955 + 0.02 * rng.random((N, 128, C, 4))) * 2.0 ** 30
    x[:, :8] = 0
    x[:, 13] = -240 * 2.0 ** 22
    x[:, 14] = -249 * 2.0 ** 22
    x[:, 15] = 0
    x[o == 3] = 2.0 ** -30
    size = np.where(o == 3, 2.0 ** -30, 2.0 ** 30)
    a = np.stack([rng.permutation(8) % 2 * 2.0 - 1.0 for r in range(N)]) * size[:, None]
    u = d["u"].reshape(N, 128, 128, 4)
    u[:, :, ::16] = a.astype(np.float32).astype(BF)[:, None, :, None]
    v = rng.choice([-1.0, 1.0], (N, 128, 512)) * size[:, None, None]
    t = rng.integers(0, C, (N, 8, C))
    t[o == 0] = C - 1
    t[o == 1] = 0
    t[o == 2] = rng.integers(0, 2, (8, C)) * (C - 1)
    k = rng.integers(0, C, (N, 8, 2 * C))
    k[e == 0] = C - 1
    k[e == 1] = 0
    k[e == 1, 7] = C - 1
    k[e == 2] = np.arange(2 * C) % 2 * (C - 1)
    w = np.zeros((N, 128, 4, 128, 4), np.float32)
    i = np.arange(128)
    for b in range(4):
        w[:, i, b, i, b] = np.where(o == 3, 16.0, -0.25)[:, None]
        for r in range(N):
            if o[r] < 3:
                w[r, :8, b, :8, b] = 64 * np.eye(8)
                w[r, 13:16, b, 13:16, b] = [[0, 0, -64], [0, 0, 64], [0, 0, 0]]
    return {"x": x.astype(np.float32).reshape(N, 128, 4 * C).astype(BF), "u": u.reshape(N, 128, 512), "v": v.astype(np.float32).astype(BF), **stored(k, t), **weights(rng, w.astype(BF))}
def setup_inputs_spread(rng):
    d = setup_inputs(rng)
    d["x"] = big(wide(rng, N, 128, 4 * C, cols=6))
    return d
def check_inputs(d):
    b = []
    for k in ("x", "u", "v"):
        a = np.abs(d[k].astype(np.float32))
        if not (np.isfinite(a).all() and ((a == 0) | (a >= 2.0 ** -30) & (a <= 2.0 ** 30)).all()): b.append("a value of " + k)
    for k in ("gl", "ht"):
        if not ((d[k] >= 0) & (d[k] < C)).all(): b.append("an entry of " + k)
    none, least, most = [emit(mx_ref.quantize(np.full((128, 16), k, np.float32).astype(BF)))[1][0, 0] for k in (0.0, 2.0 ** -30, 2.0 ** 30)]
    for r in range(N):
        if ((d["wc"][r] == 0x7F) | (d["wc"][r] == 0xFF)).any(): b.append("wc: a code that is no number")
        s = mx_ref.live(d["ws"][r])
        if ((s != none) & ((s < least) | (s > most))).any(): b.append("ws: a scale out of range")
        if (((d["wc"][r].reshape(16, 8, 512, 4) & 0x7F) != 0) & (s == none)[:, None, :, None]).any(): b.append("wc: a code other than zero under the scale of zeros")
    return b
def reference(x, u, v, gl, ht, wc, ws):
    qu = [mx_ref.quantize(u[r]) for r in range(N)]
    lay = [pk(wc[r], ws[r]) for r in range(N)]
    guest, host = [gentries(gl[r]) for r in range(N)], [gentries(ht[r]) for r in range(N)]
    now = [x[r] for r in range(N)]
    y, pl = np.zeros((N, 128, C), np.float32), np.zeros((N, 8, C), np.float32)
    for step in STEP:
        q = [mx_ref.quantize(now[r]) for r in range(N)]
        bit = [(mx_ref.matmul(qu[r], q[r])[::16] > 0).astype(np.int64) for r in range(N)]
        made = []
        for r in range(N):
            p = r ^ step
            at, there = np.zeros((9, C), np.int64), np.zeros((8, C), np.int64)
            at[0] = np.arange(C)
            for g in range(8):
                there[g] = host[p][g][at[g]]
                at[g + 1] = guest[r][g][2 * at[g] + bit[p][g][there[g]]]
            far = gcols(decode(q[p]).astype(BF), there)
            z = mx_ref.quantize(np.maximum(gcols(now[r], at[:8]).astype(np.float32), far.astype(np.float32)).astype(BF))
            made.append(tile([mx_ref.matmul(pick(lay[r], np.arange(128 * b, 128 * b + 128)), z) * np.float32(0.015625) + now[r][:, b::4].astype(np.float32) for b in range(4)]))
            pl[r] = at[1:]
        now = made
    oc, osc = np.zeros((N, 128, 4 * C), np.uint8), np.zeros((N, 16, C), np.uint8)
    for r in range(N):
        q = mx_ref.quantize(now[r])
        y[r] = mx_ref.matmul(mx_ref.quantize(v[r]), q)
        oc[r], osc[r] = emit(q)
    return {"y": y, "pl": pl, "oc": oc, "osc": osc}

@@ -1,0 +1,386 @@
+from concourse.bass import DstId, RemoteDMATransfer
+from concourse.mybir import dt, AluOpType, ActivationFunctionType
+
+C = 448
+STEPS = (1, 2, 3)
+CH = ((0, 224), (224, 448))
+BIG = 524288.0
+ALU = AluOpType
+COPY = ActivationFunctionType.Copy
+F8, U8, BF, F32, I32, U16 = "float8_e4m3fn_x4", "uint8", "bfloat16", "float32", "int32", "uint16"
+
+SCRATCH = {
+    "gli": ("sbuf", [128, 56], I32), "hti": ("sbuf", [128, 28], I32),
+    "wt": ("sbuf", [128, 96], F32), "tg": ("sbuf", [128, 128], F32), "tg2": ("sbuf", [128, 128], F32),
+    "th": ("sbuf", [128, 64], F32), "th2": ("sbuf", [128, 64], F32),
+    "gs": ("sbuf", [128, 112], U16), "hx": ("sbuf", [128, 56], U16), "hl": ("sbuf", [128, 112], U16),
+    "ut": ("sbuf", [128, 512], BF), "vt": ("sbuf", [128, 512], BF), "ec": ("sbuf", [128, 2048], BF),
+    "qu": ("sbuf", [128, 128], F8), "qus": ("sbuf", [128, 128], U8),
+    "qp": ("sbuf", [128, 256], F8), "qps": ("sbuf", [128, 256], U8),
+    "qv": ("sbuf", [128, 128], F8), "qvs": ("sbuf", [128, 128], U8),
+    "qe": ("sbuf", [128, 512], F8), "qes": ("sbuf", [128, 512], U8),
+    "qw": ("sbuf", [128, 512], F8), "qws": ("sbuf", [128, 512], U8),
+    "uli": ("sbuf", [128, 16], I32), "ul": ("sbuf", [128, 16], U16),
+    "pi": ("sbuf", [128, 1], I32), "lo": ("sbuf", [128, 1], I32), "lof": ("sbuf", [128, 1], F32),
+    "hi": ("sbuf", [128, 1], I32), "off": ("sbuf", [128, 1], F32),
+    "m16": ("sbuf", [128, 16], F32), "da": ("sbuf", [128, 16], F32), "db": ("sbuf", [128, 16], F32),
+    "dc": ("sbuf", [128, 16], F32), "dd": ("sbuf", [128, 16], F32), "de": ("sbuf", [128, 16], F32),
+    "d": ("sbuf", [128, 448], F32), "idl": ("sbuf", [128, 28], I32), "pat": ("sbuf", [128, 896], F32),
+    "wb": ("sbuf", [128, 1792], F32),
+    "b1": ("sbuf", [128, 448], F32), "b2": ("sbuf", [128, 448], F32), "t2": ("sbuf", [128, 448], F32),
+    "t1": ("sbuf", [128, 448], I32), "n1": ("sbuf", [128, 448], I32),
+    "s2": ("sbuf", [128, 448], F32), "s3": ("sbuf", [128, 448], F32), "s4": ("sbuf", [128, 448], F32),
+    "o5": ("sbuf", [128, 448], F32), "s5": ("sbuf", [128, 448], F32),
+    "i2": ("sbuf", [128, 28], I32), "j2": ("sbuf", [128, 28], I32), "l1": ("sbuf", [128, 28], U16),
+    "l2": ("sbuf", [128, 28], U16), "l3": ("sbuf", [128, 28], U16),
+    "nat": ("sbuf", [128, 896], F32), "nsc": ("sbuf", [128, 448], F32),
+    "natb": ("sbuf", [128, 896], F32), "nscb": ("sbuf", [128, 448], F32),
+    "tmp": ("sbuf", [128, 1792], F32), "x64": ("sbuf", [128, 1792], BF),
+    "o8": ("sbuf", [128, 448], F32), "s8": ("sbuf", [128, 448], F32), "l8": ("sbuf", [128, 28], U16), "r8": ("sbuf", [128, 28], U16),
+    "p7": ("sbuf", [128, 448], F32), "p8": ("sbuf", [128, 448], F32), "yb": ("sbuf", [128, 448], F32),
+    "pa": ("psum", [128, 2048], F32), "pb": ("psum", [128, 2048], F32),
+}
+for _k in range(4):
+    SCRATCH["x%d" % _k] = ("sbuf", [128, 1792], BF)
+    SCRATCH["qx%d" % _k] = ("sbuf", [128, 448], F8)
+    SCRATCH["qxs%d" % _k] = ("sbuf", [128, 448], U8)
+for _k in STEPS:
+    SCRATCH["h%d" % _k] = ("sbuf", [128, 1792], BF)
+    SCRATCH["m%d" % _k] = ("sbuf", [128, 1792], BF)
+    SCRATCH["z%d" % _k] = ("sbuf", [128, 1792], BF)
+    for _n in ("qh", "hc", "qz"):
+        SCRATCH["%s%d" % (_n, _k)] = ("sbuf", [128, 448], F8)
+    for _n in ("qhs", "hcs", "qzs"):
+        SCRATCH["%s%d" % (_n, _k)] = ("sbuf", [128, 448], U8)
+    for _n in ("vl", "vr"):
+        SCRATCH["%s%d" % (_n, _k)] = ("sbuf", [128, 28], U16)
+    SCRATCH["gr%d" % _k] = ("sbuf", [128, 112], U16)
+    for _n in ("ea", "eb"):
+        SCRATCH["%s%d" % (_n, _k)] = ("sbuf", [128, 448], F32)
+SEMAPHORES = ["v", "s", "t", "p", "rl", "k8", "dgl", "dht", "dx0", "dx1", "du", "dw", "dv", "oo", "os_", "oy", "op_"]
+for _k in STEPS:
+    SEMAPHORES += ["g%d" % _k, "k%d" % _k, "c%da" % _k, "c%db" % _k]
+
+
+def rank_program(g, core, T, topo):
+    rank = T.rank_of(core)
+    if rank is None:
+        return
+    queue = {"v": g.vector, "s": g.scalar, "t": g.tensor, "p": g, "y": g.sync}
+    total, log = {}, {}
+    seen = dict((q, {}) for q in queue)
+
+    def A(name, a=0, b=None, step=1, p=None, cast=None, by=None):
+        t = T[name]
+        b = t.shape[1] if b is None else b
+        lo, hi = p if p else (0, 128)
+        reg = [(name, lo, hi, a, b)]
+        if name in ("pa", "pb"):
+            reg = [(name, 0, 128, a // 512 * 512, (b + 511) // 512 * 512)]
+        if p:
+            v = t[lo:hi, a:b:step] if step > 1 else t[lo:hi, a:b]
+        else:
+            v = t[:, a:b:step] if step > 1 else t[:, a:b]
+        if cast is not None:
+            v = v.bitcast(cast)
+        if by is not None:
+            v = v.indirect(by[0])
+            reg = reg + by[1]
+        return v, reg
+
+    def touch(r, s):
+        return r[0] == s[0] and r[1] < s[2] and s[1] < r[2] and r[3] < s[4] and s[3] < r[4]
+
+    def waits(q, reads, writes):
+        need = {}
+        for regs, wr in ((reads, False), (writes, True)):
+            for r in regs:
+                for reg, was, sem, val in log.get(r[0], []):
+                    if touch(r, reg) and (wr or was or r[0] in ("pa", "pb")):
+                        need[sem] = max(need.get(sem, 0), total[sem] if val is None else val)
+        for sem in sorted(need):
+            if seen[q].get(sem, 0) < need[sem]:
+                queue[q].wait_ge(T.sem[sem], need[sem])
+                seen[q][sem] = need[sem]
+
+    def note(reads, writes, sem, val):
+        for r in writes:
+            old = log.get(r[0], [])
+            log[r[0]] = [e for e in old if not (r[1] <= e[0][1] and e[0][2] <= r[2] and r[3] <= e[0][3] and e[0][4] <= r[4])]
+            log[r[0]].append((r, True, sem, val))
+        for r in reads:
+            log.setdefault(r[0], []).append((r, False, sem, val))
+
+    def run(q, call, outs, ins, extra=()):
+        reads = [r for o in list(ins) + list(extra) for r in o[1]]
+        writes = [r for o in outs for r in o[1]]
+        waits(q, reads, writes)
+        call().then_inc(T.sem[q], 1)
+        total[q] = total.get(q, 0) + 1
+        note(reads, writes, q, total[q])
+
+    def dma(q, out, in_, sem):
+        waits(q, in_[1], out[1])
+        queue[q].dma_start(out[0], in_[0]).then_inc(T.sem[sem], 16)
+        total[sem] = total.get(sem, 0) + 16
+        note(in_[1], out[1], sem, None)
+
+    def ext(view):
+        return view, []
+
+    def send(step, out, in_, sem):
+        dst = core_of(step)
+        waits("p", in_[1], [])
+        rid, pid, _ = topo.addr(dst)
+        g.remote_dma(out[0], in_[0], T.sem[sem], T.sem.rl, pid, rid, topo.mask(core, dst))
+        total["rl"] = total.get("rl", 0) + len(topo.engines(core, dst))
+
+    def core_of(step):
+        return T.cores[rank ^ step]
+
+    def arrives(step, out, sem):
+        total[sem] = total.get(sem, 0) + len(topo.engines(core_of(step), core))
+        note([], out[1], sem, None)
+
+    def copy(out, in_, q="v"):
+        if q == "v":
+            run("v", lambda: g.vector.tensor_copy(out[0], in_[0]), [out], [in_])
+        else:
+            run("s", lambda: g.scalar.activation(out[0], in_[0], COPY), [out], [in_])
+
+    def scaled(out, in_, c):
+        run("s", lambda: g.scalar.activation(out[0], in_[0], COPY, scale=c), [out], [in_])
+
+    def ts(out, in_, a, op0, b=None, op1=None):
+        col = [a] if isinstance(a, tuple) else []
+        a0 = a[0] if col else a
+        if op1 is None:
+            run("v", lambda: g.vector.tensor_scalar(out[0], in_[0], a0, None, op0), [out], [in_] + col)
+        else:
+            run("v", lambda: g.vector.tensor_scalar(out[0], in_[0], a0, b, op0, op1), [out], [in_] + col)
+
+    def tt(out, a, b, op):
+        run("v", lambda: g.vector.tensor_tensor(out[0], a[0], b[0], op), [out], [a, b])
+
+    def fill(out, c):
+        run("v", lambda: g.vector.memset(out[0], c), [out], [])
+
+    def turn(out, in_):
+        run("v", lambda: g.vector.transpose(out[0], in_[0]), [out], [in_])
+
+    def quant(q, s, in_):
+        run("v", lambda: g.vector.quantize_mx(q[0], s[0], in_[0]), [q, s], [in_])
+
+    def mm(out, l, ls, r, rs):
+        run("t", lambda: g.tensor.matmul_mx(out[0], l[0], ls[0], r[0], rs[0], True, True), [out], [l, ls, r, rs])
+
+    def iota(out, pattern, base, cm, f=False):
+        if f:
+            run("p", lambda: g.iota(out[0], pattern, base, cm, allow_small_or_imprecise_dtypes=True), [out], [])
+        else:
+            run("p", lambda: g.iota(out[0], pattern, base, cm), [out], [])
+
+    def scan(out, in_):
+        d = A("d")
+        run("v", lambda: g.vector.tensor_tensor_scan(out[0], in_[0], d[0], -BIG, ALU.max, ALU.add), [out], [in_, d])
+
+    def wrapped(name, p=None):
+        return A(name, 15, 448, 16, p)
+
+    dma("y", A("gli"), ext(T.gl[:, :]), "dgl")
+    dma("s", A("hti"), ext(T.ht[:, :]), "dht")
+    for k, (a, b) in enumerate(CH):
+        dma("s" if k == 0 else "y", A("x0", 4 * a, 4 * b), ext(T.x[:, 4 * a:4 * b]), "dx%d" % k)
+    dma("y", A("ut"), ext(T.u[:, :]), "du")
+    dma("y", A("qws"), ext(T.ws[:, :]), "dw")
+    dma("y", A("qw", cast=dt.uint8), ext(T.wc[:, :]), "dw")
+    dma("y", A("vt"), ext(T.v[:, :]), "dv")
+
+    fill(A("wt"), 0.0)
+    iota(A("m16"), [[1, 16]], 0, 0, True)
+    iota(A("pi"), [[0, 1]], 0, 1)
+    iota(A("uli"), [[16, 2], [32, 4], [0, 2]], 0, 0)
+    iota(A("idl"), [[16, 28]], 0, 1)
+    iota(A("wb", 0, 448), [[1, 448]], 0, 0, True)
+    fill(A("ec"), 1.0)
+    fill(A("pat", 0, 896, 2), 1024.0)
+    fill(A("pat", 1, 896, 2), 1.0)
+    fill(A("l2"), 0)
+    copy(A("wt", 0, 56), A("gli"))
+    turn(A("tg", 0, 64), A("wt", 0, 64))
+    turn(A("tg", 64, 128), A("wt", 0, 64))
+    for k in (0, 32):
+        copy(A("tg", k + 16, k + 32), A("tg", k, k + 16))
+        copy(A("tg", 64 + k, 64 + k + 16), A("tg", 64 + k + 16, 64 + k + 32))
+    turn(A("tg2"), A("tg"))
+    copy(A("gs", 0, 56), A("tg2", 0, 56))
+    copy(A("gs", 56, 112), A("tg2", 64, 120))
+    send(1, A("gr1"), A("gs"), "g1")
+    run("p", lambda: g.affine_select(T.ec[:, :], T.ec[:, :], [[1, 4], [-1, 512]], ALU.is_equal, 0.0, 0, 4), [A("ec")], [A("ec")])
+    for s in (2, 3):
+        send(s, A("gr%d" % s), A("gs"), "g%d" % s)
+    for s in STEPS:
+        arrives(s, A("gr%d" % s), "g%d" % s)
+    for t in range(4):
+        ts(A("hl", 28 * t, 28 * t + 28), A("hti"), 4.0, ALU.mult, float(t), ALU.add)
+    copy(A("ul"), A("uli"))
+    quant(A("qu"), A("qus"), A("ut"))
+    ul = A("ul")
+    copy(A("qp", cast=dt.uint32), A("qu", cast=dt.uint32, by=ul))
+    copy(A("qps"), A("qus", by=ul))
+    copy(A("wt", 64, 92), A("hti"))
+    turn(A("th", 0, 32), A("wt", 64, 96))
+    turn(A("th", 32, 64), A("wt", 64, 96))
+    copy(A("th", 16, 32), A("th", 0, 16))
+    copy(A("th", 32, 48), A("th", 48, 64))
+    turn(A("th2"), A("th"))
+    copy(A("hx", 0, 28), A("th2", 0, 28))
+    copy(A("hx", 28, 56), A("th2", 32, 60))
+    ts(A("lo"), A("pi"), 15, ALU.bitwise_and)
+    copy(A("lof"), A("lo"))
+    ts(A("hi"), A("pi"), 4, ALU.logical_shift_right, 1, ALU.bitwise_and)
+    ts(A("off"), A("hi"), 448.0, ALU.mult, BIG, ALU.add)
+    ts(A("da"), A("m16"), A("lof"), ALU.is_ge)
+    ts(A("db"), A("m16"), A("lof"), ALU.is_equal)
+    ts(A("dc"), A("m16"), 15.0, ALU.is_equal, -2.0, ALU.mult)
+    tt(A("dd"), A("da"), A("db"), ALU.add)
+    tt(A("de"), A("dd"), A("dc"), ALU.add)
+    ts(A("d", 0, 16), A("de"), -1.0, ALU.add, BIG, ALU.mult)
+    w = 16
+    while w < C:
+        n = min(w, C - w)
+        copy(A("d", w, w + n), A("d", 0, n))
+        w += n
+
+    def table(s, wave, fused):
+        lst = A("gr%d" % s, 56 * wave, 56 * wave + 56)
+        e = A("%s%d" % ("ab"[wave] and ("ea", "eb")[wave], s))
+        nat, nsc = (("nat", "nsc"), ("natb", "nscb"))[wave]
+        if fused:
+            tt(A(nat), A("wb", 0, 448, by=lst), A("pat"), ALU.mult)
+            return lambda: tt(e, A(nat, 0, 896, 2), A(nat, 1, 896, 2), ALU.add)
+        copy(A(nat), A("wb", 0, 448, by=lst), "s")
+        scaled(A(nsc), A(nat, 0, 896, 2), 1024.0)
+        return lambda: tt(e, A(nsc), A(nat, 1, 896, 2), ALU.add)
+
+    pend = []
+    for s in STEPS:
+        k = "%d" % s
+        xo, xn = "x%d" % (s - 1), "x" + k
+        qx, qxs = "qx%d" % (s - 1), "qxs%d" % (s - 1)
+        first = s == 1
+
+        def host_gather(a, b):
+            for t in range(4):
+                copy(A("h" + k, 4 * a + t, 4 * b, 4), A(xo, by=A("hl", 28 * t + a // 16, 28 * t + b // 16)), "s")
+
+        def host_send(c):
+            a, b = CH[c]
+            quant(A("qh" + k, a, b), A("qhs" + k, a, b), A("h" + k, 4 * a, 4 * b))
+            sem = "c" + k + "ab"[c]
+            send(s, A("hc" + k, a, b, cast=dt.uint8), A("qh" + k, a, b, cast=dt.uint8), sem)
+            send(s, A("hcs" + k, a, b), A("qhs" + k, a, b), sem)
+            arrives(s, A("hc" + k, a, b), sem)
+            arrives(s, A("hcs" + k, a, b), sem)
+
+        for a, b in CH:
+            quant(A(qx, a, b), A(qxs, a, b), A(xo, 4 * a, 4 * b))
+        for a, b in CH:
+            host_gather(a, b)
+        mm(A("pa", 0, 448), A("qp", 0, 128), A("qps", 0, 128), A(qx), A(qxs))
+        mm(A("pa", 512, 960), A("qp", 128, 256), A("qps", 128, 256), A(qx), A(qxs))
+
+        def bits(n):
+            ts(A("b2" if n == 0 else "b1"), A("pa", 512 * n, 512 * n + 448), 0.0, ALU.is_gt, 2.0 ** -10, ALU.max)
+
+        bits(0)
+        if first:
+            bits(1)
+            host_send(0)
+            host_send(1)
+            add1 = table(1, 1, False)
+            table(1, 0, True)()
+        tt(A("t2"), A("b2", by=A("hx", 0, 28)), A("ea" + k), ALU.mult)
+        scan(A("s2"), A("t2"))
+        copy(A("i2"), wrapped("s2"))
+        ts(A("j2"), A("i2"), 1023, ALU.bitwise_and)
+        copy(A("l1"), A("j2"))
+        copy(A("wb", 448, 896), A("wb", 0, 448, by=A("l1")), "s")
+        if first:
+            add1()
+        else:
+            host_send(0)
+            bits(1)
+        tt(A("t1"), A("b1", by=A("hx", 28, 56)), A("eb" + k), ALU.mult)
+        ts(A("n1"), A("t1"), 1023, ALU.bitwise_and)
+        if not first:
+            host_send(1)
+        scaled(A("x64"), A(xo), 64.0)
+        if s < 3:
+            pend = [table(s + 1, 0, False), table(s + 1, 1, False)]
+        copy(A("wb", 896, 1344), A("n1", by=A("l1")))
+        scan(A("s3"), A("wb", 896, 1344))
+        ts(A("l2", p=(32, 64)), wrapped("s3", (0, 32)), BIG + 896.0, ALU.add)
+        ts(A("l2", p=(96, 128)), wrapped("s3", (64, 96)), A("off", p=(64, 96)), ALU.add)
+        copy(A("wb", 1344, 1792), A("wb", 0, 1344, by=A("l2")))
+        copy(A("l3", p=(0, 32)), A("j2", p=(0, 32)))
+        copy(A("l3", p=(0, 16)), A("idl", p=(0, 16)))
+        ts(A("l3", p=(32, 64)), wrapped("s3", (0, 32)), A("off", p=(0, 32)), ALU.add)
+        scan(A("s4"), A("wb", 1344, 1792))
+        ts(A("l3", p=(64, 96)), wrapped("s4", (32, 64)), A("off", p=(32, 64)), ALU.add)
+        ts(A("l3", p=(96, 128)), wrapped("s4", (32, 64)), BIG + 1344.0, ALU.add)
+        copy(A("o5"), A("wb", by=A("l3")))
+        scan(A("s5"), A("o5"))
+        ts(A("vl" + k), wrapped("s5"), BIG, ALU.add)
+        send(s, A("vr" + k), A("vl" + k), "k" + k)
+        arrives(s, A("vr" + k), "k" + k)
+        if s == 3:
+            copy(A("o8"), A("n1", by=A("vl" + k)))
+            scan(A("s8"), A("o8"))
+            ts(A("l8"), wrapped("s8"), BIG, ALU.add)
+            send(s, A("r8"), A("l8"), "k8")
+            arrives(s, A("r8"), "k8")
+        if first:
+            quant(A("qe"), A("qes"), A("ec"))
+            quant(A("qv"), A("qvs"), A("vt"))
+        for add in pend:
+            add()
+        pend = []
+        for c, (a, b) in enumerate(CH):
+            ps = "pa" if c == 0 else "pb"
+            for t in range(4):
+                mm(A(ps, 512 * t, 512 * t + b - a), A("qe", 128 * t, 128 * t + 128), A("qes", 128 * t, 128 * t + 128),
+                   A("hc" + k, a, b), A("hcs" + k, a, b))
+            for t in range(4):
+                tt(A("m" + k, 448 * t + a, 448 * t + b), A(xo, 4 * a + t, 4 * b, 4), A(ps, 512 * t, 512 * t + b - a), ALU.max)
+        for c, (a, b) in enumerate(CH):
+            ps = "pa" if c == 0 else "pb"
+            by = A("vr" + k, a // 16, b // 16)
+            for t in (0, 2, 1, 3):
+                copy(A("z" + k, 4 * a + t, 4 * b, 4), A("m" + k, 448 * t, 448 * t + 448, by=by), "v" if t < 2 else "s")
+            quant(A("qz" + k, a, b), A("qzs" + k, a, b), A("z" + k, 4 * a, 4 * b))
+            for t in range(4):
+                mm(A(ps, 512 * t, 512 * t + b - a), A("qw", 128 * t, 128 * t + 128), A("qws", 128 * t, 128 * t + 128),
+                   A("qz" + k, a, b), A("qzs" + k, a, b))
+        for c, (a, b) in enumerate(CH):
+            ps = "pa" if c == 0 else "pb"
+            for t in range(4):
+                tt(A("tmp", 448 * t + a, 448 * t + b), A(ps, 512 * t, 512 * t + b - a), A("x64", 4 * a + t, 4 * b, 4), ALU.add)
+                scaled(A(xn, 4 * a + t, 4 * b, 4), A("tmp", 448 * t + a, 448 * t + b), 2.0 ** -6)
+
+    for c, (a, b) in enumerate(CH):
+        quant(A("qx3", a, b), A("qxs3", a, b), A("x3", 4 * a, 4 * b))
+        mm(A("pa", 512 * c, 512 * c + b - a), A("qv"), A("qvs"), A("qx3", a, b), A("qxs3", a, b))
+    copy(A("p7"), A("wb", 0, 448, by=A("vr3")), "s")
+    dma("y", ext(T.pl[0:7, :]), (T.p7[16:128:16, :], A("p7")[1]), "op_")
+    copy(A("p8"), A("wb", 0, 448, by=A("r8")), "s")
+    dma("y", ext(T.pl[7:8, :]), A("p8", p=(112, 113)), "op_")
+    for c, (a, b) in enumerate(CH):
+        copy(A("yb", a, b), A("pa", 512 * c, 512 * c + b - a))
+        dma("y", ext(T.oc[:, 4 * a:4 * b]), A("qx3", a, b, cast=dt.uint8), "oo")
+        dma("y" if c else "s", ext(T.y[:, a:b]), A("yb", a, b), "oy")
+    for i in range(4):
+        dma("s", ext(T.osc[4 * i:4 * i + 4, :]), A("qxs3", p=(32 * i, 32 * i + 4)), "os_")
+    for sem in sorted(total):
+        if seen["p"].get(sem, 0) < total[sem]:
+            g.wait_ge(T.sem[sem], total[sem])

@@ -3,7 +3,9 @@ from concourse.mybir import dt, AluOpType, ActivationFunctionType
 
 C = 448
 STEPS = (1, 2, 3)
-CH = ((0, 224), (224, 448))
+CHH = ((0, 224), (224, 448))
+CHZ = ((0, 128), (128, 288), (288, 448))
+CHX = ((0, 288), (288, 448))
 BIG = 524288.0
 ALU = AluOpType
 COPY = ActivationFunctionType.Copy
@@ -74,9 +76,9 @@ def rank_program(g, core, T, topo):
         t = T[name]
         b = t.shape[1] if b is None else b
         lo, hi = p if p else (0, 128)
-        reg = [(name, lo, hi, a, b)]
+        reg = [(name, lo, hi, a, b, step)]
         if name in ("pa", "pb"):
-            reg = [(name, 0, 128, a // 512 * 512, (b + 511) // 512 * 512)]
+            reg = [(name, 0, 128, a // 512 * 512, (b + 511) // 512 * 512, 1)]
         if p:
             v = t[lo:hi, a:b:step] if step > 1 else t[lo:hi, a:b]
         else:
@@ -89,7 +91,12 @@ def rank_program(g, core, T, topo):
         return v, reg
 
     def touch(r, s):
-        return r[0] == s[0] and r[1] < s[2] and s[1] < r[2] and r[3] < s[4] and s[3] < r[4]
+        apart = r[5] == s[5] and (r[3] - s[3]) % r[5] != 0
+        return r[1] < s[2] and s[1] < r[2] and r[3] < s[4] and s[3] < r[4] and not apart
+
+    def covers(r, s):
+        same = r[5] == 1 or r[5] == s[5] and (r[3] - s[3]) % r[5] == 0
+        return r[1] <= s[1] and s[2] <= r[2] and r[3] <= s[3] and s[4] <= r[4] and same
 
     def waits(q, reads, writes):
         need = {}
@@ -105,14 +112,12 @@ def rank_program(g, core, T, topo):
 
     def note(reads, writes, sem, val):
         for r in writes:
-            old = log.get(r[0], [])
-            log[r[0]] = [e for e in old if not (r[1] <= e[0][1] and e[0][2] <= r[2] and r[3] <= e[0][3] and e[0][4] <= r[4])]
-            log[r[0]].append((r, True, sem, val))
+            log[r[0]] = [e for e in log.get(r[0], []) if not covers(r, e[0])] + [(r, True, sem, val)]
         for r in reads:
             log.setdefault(r[0], []).append((r, False, sem, val))
 
-    def run(q, call, outs, ins, extra=()):
-        reads = [r for o in list(ins) + list(extra) for r in o[1]]
+    def run(q, call, outs, ins):
+        reads = [r for o in ins for r in o[1]]
         writes = [r for o in outs for r in o[1]]
         waits(q, reads, writes)
         call().then_inc(T.sem[q], 1)
@@ -128,6 +133,9 @@ def rank_program(g, core, T, topo):
     def ext(view):
         return view, []
 
+    def core_of(step):
+        return T.cores[rank ^ step]
+
     def send(step, out, in_, sem):
         dst = core_of(step)
         waits("p", in_[1], [])
@@ -135,11 +143,21 @@ def rank_program(g, core, T, topo):
         g.remote_dma(out[0], in_[0], T.sem[sem], T.sem.rl, pid, rid, topo.mask(core, dst))
         total["rl"] = total.get("rl", 0) + len(topo.engines(core, dst))
 
-    def core_of(step):
-        return T.cores[rank ^ step]
+    def send_both():
+        mv = []
+        waits("p", A("gs")[1], [])
+        for j, st in enumerate((2, 3)):
+            dst = core_of(st)
+            rid, pid, _ = topo.addr(dst)
+            eng = topo.engines(core, dst)
+            mine = eng[len(eng) // 2 * j:len(eng) // 2 * (j + 1)]
+            mv.append(RemoteDMATransfer(dst_ids=[DstId(rid=rid, pnc=pid)], dma_engine_mask=sum(1 << e for e in mine),
+                                        remote_sem=T.sem["g%d" % st], src=T.gs[:, :], dst=T["gr%d" % st][:, :]))
+            total["rl"] = total.get("rl", 0) + len(mine)
+        g.remote_dma_fused(mv, local_sem=T.sem.rl)
 
-    def arrives(step, out, sem):
-        total[sem] = total.get(sem, 0) + len(topo.engines(core_of(step), core))
+    def arrives(step, out, sem, part=1):
+        total[sem] = total.get(sem, 0) + len(topo.engines(core_of(step), core)) // part
         note([], out[1], sem, None)
 
     def copy(out, in_, q="v"):
@@ -187,9 +205,12 @@ def rank_program(g, core, T, topo):
     def wrapped(name, p=None):
         return A(name, 15, 448, 16, p)
 
+    def bank(c, t, n):
+        return A(("pa", "pb")[c % 2], 512 * t, 512 * t + n)
+
     dma("y", A("gli"), ext(T.gl[:, :]), "dgl")
     dma("s", A("hti"), ext(T.ht[:, :]), "dht")
-    for k, (a, b) in enumerate(CH):
+    for k, (a, b) in enumerate(CHX):
         dma("s" if k == 0 else "y", A("x0", 4 * a, 4 * b), ext(T.x[:, 4 * a:4 * b]), "dx%d" % k)
     dma("y", A("ut"), ext(T.u[:, :]), "du")
     dma("y", A("qws"), ext(T.ws[:, :]), "dw")
@@ -202,10 +223,23 @@ def rank_program(g, core, T, topo):
     iota(A("uli"), [[16, 2], [32, 4], [0, 2]], 0, 0)
     iota(A("idl"), [[16, 28]], 0, 1)
     iota(A("wb", 0, 448), [[1, 448]], 0, 0, True)
-    fill(A("ec"), 1.0)
-    fill(A("pat", 0, 896, 2), 1024.0)
-    fill(A("pat", 1, 896, 2), 1.0)
+    ts(A("lo"), A("pi"), 15, ALU.bitwise_and)
+    ts(A("hi"), A("pi"), 4, ALU.logical_shift_right, 1, ALU.bitwise_and)
+    ts(A("dc"), A("m16"), 15.0, ALU.is_equal, -2.0, ALU.mult)
+    copy(A("lof"), A("lo"))
+    ts(A("off"), A("hi"), 448.0, ALU.mult, BIG, ALU.add)
+    copy(A("ul"), A("uli"))
+    ts(A("da"), A("m16"), A("lof"), ALU.is_ge)
+    ts(A("db"), A("m16"), A("lof"), ALU.is_equal)
     fill(A("l2"), 0)
+    tt(A("dd"), A("da"), A("db"), ALU.add)
+    tt(A("de"), A("dd"), A("dc"), ALU.add)
+    ts(A("d", 0, 16), A("de"), -1.0, ALU.add, BIG, ALU.mult)
+    w = 16
+    while w < C:
+        n = min(w, C - w)
+        copy(A("d", w, w + n), A("d", 0, n))
+        w += n
     copy(A("wt", 0, 56), A("gli"))
     turn(A("tg", 0, 64), A("wt", 0, 64))
     turn(A("tg", 64, 128), A("wt", 0, 64))
@@ -216,18 +250,16 @@ def rank_program(g, core, T, topo):
     copy(A("gs", 0, 56), A("tg2", 0, 56))
     copy(A("gs", 56, 112), A("tg2", 64, 120))
     send(1, A("gr1"), A("gs"), "g1")
-    run("p", lambda: g.affine_select(T.ec[:, :], T.ec[:, :], [[1, 4], [-1, 512]], ALU.is_equal, 0.0, 0, 4), [A("ec")], [A("ec")])
-    for s in (2, 3):
-        send(s, A("gr%d" % s), A("gs"), "g%d" % s)
     for s in STEPS:
-        arrives(s, A("gr%d" % s), "g%d" % s)
+        arrives(s, A("gr%d" % s), "g%d" % s, 1 if s == 1 else 2)
     for t in range(4):
         ts(A("hl", 28 * t, 28 * t + 28), A("hti"), 4.0, ALU.mult, float(t), ALU.add)
-    copy(A("ul"), A("uli"))
+    fill(A("ec"), 1.0)
+    run("p", lambda: g.affine_select(T.ec[:, :], T.ec[:, :], [[1, 4], [-1, 512]], ALU.is_equal, 0.0, 0, 4), [A("ec")], [A("ec")])
     quant(A("qu"), A("qus"), A("ut"))
     ul = A("ul")
+    copy(A("qps"), A("qus", by=ul), "s")
     copy(A("qp", cast=dt.uint32), A("qu", cast=dt.uint32, by=ul))
-    copy(A("qps"), A("qus", by=ul))
     copy(A("wt", 64, 92), A("hti"))
     turn(A("th", 0, 32), A("wt", 64, 96))
     turn(A("th", 32, 64), A("wt", 64, 96))
@@ -236,46 +268,27 @@ def rank_program(g, core, T, topo):
     turn(A("th2"), A("th"))
     copy(A("hx", 0, 28), A("th2", 0, 28))
     copy(A("hx", 28, 56), A("th2", 32, 60))
-    ts(A("lo"), A("pi"), 15, ALU.bitwise_and)
-    copy(A("lof"), A("lo"))
-    ts(A("hi"), A("pi"), 4, ALU.logical_shift_right, 1, ALU.bitwise_and)
-    ts(A("off"), A("hi"), 448.0, ALU.mult, BIG, ALU.add)
-    ts(A("da"), A("m16"), A("lof"), ALU.is_ge)
-    ts(A("db"), A("m16"), A("lof"), ALU.is_equal)
-    ts(A("dc"), A("m16"), 15.0, ALU.is_equal, -2.0, ALU.mult)
-    tt(A("dd"), A("da"), A("db"), ALU.add)
-    tt(A("de"), A("dd"), A("dc"), ALU.add)
-    ts(A("d", 0, 16), A("de"), -1.0, ALU.add, BIG, ALU.mult)
-    w = 16
-    while w < C:
-        n = min(w, C - w)
-        copy(A("d", w, w + n), A("d", 0, n))
-        w += n
 
     def table(s, wave, fused):
         lst = A("gr%d" % s, 56 * wave, 56 * wave + 56)
-        e = A("%s%d" % ("ab"[wave] and ("ea", "eb")[wave], s))
+        e = "%s%d" % (("ea", "eb")[wave], s)
         nat, nsc = (("nat", "nsc"), ("natb", "nscb"))[wave]
         if fused:
             tt(A(nat), A("wb", 0, 448, by=lst), A("pat"), ALU.mult)
-            return lambda: tt(e, A(nat, 0, 896, 2), A(nat, 1, 896, 2), ALU.add)
+            return lambda a=0, b=C: tt(A(e, a, b), A(nat, 2 * a, 2 * b, 2), A(nat, 2 * a + 1, 2 * b, 2), ALU.add)
         copy(A(nat), A("wb", 0, 448, by=lst), "s")
         scaled(A(nsc), A(nat, 0, 896, 2), 1024.0)
-        return lambda: tt(e, A(nsc), A(nat, 1, 896, 2), ALU.add)
+        return lambda a=0, b=C: tt(A(e, a, b), A(nsc, a, b), A(nat, 2 * a + 1, 2 * b, 2), ALU.add)
 
-    pend = []
+    early = late = None
     for s in STEPS:
         k = "%d" % s
         xo, xn = "x%d" % (s - 1), "x" + k
         qx, qxs = "qx%d" % (s - 1), "qxs%d" % (s - 1)
         first = s == 1
 
-        def host_gather(a, b):
-            for t in range(4):
-                copy(A("h" + k, 4 * a + t, 4 * b, 4), A(xo, by=A("hl", 28 * t + a // 16, 28 * t + b // 16)), "s")
-
         def host_send(c):
-            a, b = CH[c]
+            a, b = CHH[c]
             quant(A("qh" + k, a, b), A("qhs" + k, a, b), A("h" + k, 4 * a, 4 * b))
             sem = "c" + k + "ab"[c]
             send(s, A("hc" + k, a, b, cast=dt.uint8), A("qh" + k, a, b, cast=dt.uint8), sem)
@@ -283,49 +296,64 @@ def rank_program(g, core, T, topo):
             arrives(s, A("hc" + k, a, b), sem)
             arrives(s, A("hcs" + k, a, b), sem)
 
-        for a, b in CH:
+        def bits(n, c):
+            a, b = CHX[c]
+            w = 512 * (2 * n + c)
+            ts(A(("b2", "b1")[n], a, b), A("pa", w, w + b - a), 0.0, ALU.is_gt, 2.0 ** -10, ALU.max)
+
+        for c, (a, b) in enumerate(CHX):
             quant(A(qx, a, b), A(qxs, a, b), A(xo, 4 * a, 4 * b))
-        for a, b in CH:
-            host_gather(a, b)
-        mm(A("pa", 0, 448), A("qp", 0, 128), A("qps", 0, 128), A(qx), A(qxs))
-        mm(A("pa", 512, 960), A("qp", 128, 256), A("qps", 128, 256), A(qx), A(qxs))
-
-        def bits(n):
-            ts(A("b2" if n == 0 else "b1"), A("pa", 512 * n, 512 * n + 448), 0.0, ALU.is_gt, 2.0 ** -10, ALU.max)
-
-        bits(0)
+            if not first:
+                late(224 * c, 224 * c + 224)
+        for n in range(2):
+            for c, (a, b) in enumerate(CHX):
+                w = 512 * (2 * n + c)
+                mm(A("pa", w, w + b - a), A("qp", 128 * n, 128 * n + 128), A("qps", 128 * n, 128 * n + 128), A(qx, a, b), A(qxs, a, b))
+        for a, b in CHH:
+            for t in range(4):
+                copy(A("h" + k, 4 * a + t, 4 * b, 4), A(xo, by=A("hl", 28 * t + a // 16, 28 * t + b // 16)), "s")
+        bits(0, 0)
+        bits(0, 1)
         if first:
-            bits(1)
+            late = table(1, 1, False)
+            bits(1, 0)
+            bits(1, 1)
+            fill(A("pat", 0, 896, 2), 1024.0)
+            fill(A("pat", 1, 896, 2), 1.0)
             host_send(0)
-            host_send(1)
-            add1 = table(1, 1, False)
             table(1, 0, True)()
         tt(A("t2"), A("b2", by=A("hx", 0, 28)), A("ea" + k), ALU.mult)
+        if not first:
+            bits(1, 0)
         scan(A("s2"), A("t2"))
-        copy(A("i2"), wrapped("s2"))
-        ts(A("j2"), A("i2"), 1023, ALU.bitwise_and)
-        copy(A("l1"), A("j2"))
-        copy(A("wb", 448, 896), A("wb", 0, 448, by=A("l1")), "s")
         if first:
-            add1()
+            host_send(1)
+            send_both()
+        else:
+            bits(1, 1)
+        copy(A("i2"), wrapped("s2"))
+        if first:
+            late()
         else:
             host_send(0)
-            bits(1)
+        ts(A("j2"), A("i2"), 1023, ALU.bitwise_and)
         tt(A("t1"), A("b1", by=A("hx", 28, 56)), A("eb" + k), ALU.mult)
+        copy(A("l1"), A("j2"))
         ts(A("n1"), A("t1"), 1023, ALU.bitwise_and)
+        copy(A("wb", 448, 896), A("wb", 0, 448, by=A("l1")), "s")
         if not first:
             host_send(1)
         scaled(A("x64"), A(xo), 64.0)
         if s < 3:
-            pend = [table(s + 1, 0, False), table(s + 1, 1, False)]
+            early, late = table(s + 1, 0, False), table(s + 1, 1, False)
         copy(A("wb", 896, 1344), A("n1", by=A("l1")))
+        copy(A("l3", p=(0, 32)), A("j2", p=(0, 32)))
         scan(A("s3"), A("wb", 896, 1344))
+        copy(A("l3", p=(0, 16)), A("idl", p=(0, 16)))
         ts(A("l2", p=(32, 64)), wrapped("s3", (0, 32)), BIG + 896.0, ALU.add)
         ts(A("l2", p=(96, 128)), wrapped("s3", (64, 96)), A("off", p=(64, 96)), ALU.add)
-        copy(A("wb", 1344, 1792), A("wb", 0, 1344, by=A("l2")))
-        copy(A("l3", p=(0, 32)), A("j2", p=(0, 32)))
-        copy(A("l3", p=(0, 16)), A("idl", p=(0, 16)))
         ts(A("l3", p=(32, 64)), wrapped("s3", (0, 32)), A("off", p=(0, 32)), ALU.add)
+        copy(A("wb", 1344, 1792), A("wb", 0, 1344, by=A("l2")))
         scan(A("s4"), A("wb", 1344, 1792))
         ts(A("l3", p=(64, 96)), wrapped("s4", (32, 64)), A("off", p=(32, 64)), ALU.add)
         ts(A("l3", p=(96, 128)), wrapped("s4", (32, 64)), BIG + 1344.0, ALU.add)
@@ -343,41 +371,42 @@ def rank_program(g, core, T, topo):
         if first:
             quant(A("qe"), A("qes"), A("ec"))
             quant(A("qv"), A("qvs"), A("vt"))
-        for add in pend:
-            add()
-        pend = []
-        for c, (a, b) in enumerate(CH):
-            ps = "pa" if c == 0 else "pb"
+        if s < 3:
+            early()
+        for c, (a, b) in enumerate(CHH):
             for t in range(4):
-                mm(A(ps, 512 * t, 512 * t + b - a), A("qe", 128 * t, 128 * t + 128), A("qes", 128 * t, 128 * t + 128),
-                   A("hc" + k, a, b), A("hcs" + k, a, b))
+                mm(bank(c, t, b - a), A("qe", 128 * t, 128 * t + 128), A("qes", 128 * t, 128 * t + 128), A("hc" + k, a, b), A("hcs" + k, a, b))
             for t in range(4):
-                tt(A("m" + k, 448 * t + a, 448 * t + b), A(xo, 4 * a + t, 4 * b, 4), A(ps, 512 * t, 512 * t + b - a), ALU.max)
-        for c, (a, b) in enumerate(CH):
-            ps = "pa" if c == 0 else "pb"
+                tt(A("m" + k, 448 * t + a, 448 * t + b), A(xo, 4 * a + t, 4 * b, 4), bank(c, t, b - a), ALU.max)
+        def finish(c):
+            a, b = CHZ[c]
+            for t in range(4):
+                tt(A("tmp", 448 * t + a, 448 * t + b), bank(c, t, b - a), A("x64", 4 * a + t, 4 * b, 4), ALU.add)
+                scaled(A(xn, 4 * a + t, 4 * b, 4), A("tmp", 448 * t + a, 448 * t + b), 2.0 ** -6)
+
+        for c, (a, b) in enumerate(CHZ):
             by = A("vr" + k, a // 16, b // 16)
             for t in (0, 2, 1, 3):
                 copy(A("z" + k, 4 * a + t, 4 * b, 4), A("m" + k, 448 * t, 448 * t + 448, by=by), "v" if t < 2 else "s")
             quant(A("qz" + k, a, b), A("qzs" + k, a, b), A("z" + k, 4 * a, 4 * b))
+            if c == 2:
+                finish(0)
             for t in range(4):
-                mm(A(ps, 512 * t, 512 * t + b - a), A("qw", 128 * t, 128 * t + 128), A("qws", 128 * t, 128 * t + 128),
+                mm(bank(c, t, b - a), A("qw", 128 * t, 128 * t + 128), A("qws", 128 * t, 128 * t + 128),
                    A("qz" + k, a, b), A("qzs" + k, a, b))
-        for c, (a, b) in enumerate(CH):
-            ps = "pa" if c == 0 else "pb"
-            for t in range(4):
-                tt(A("tmp", 448 * t + a, 448 * t + b), A(ps, 512 * t, 512 * t + b - a), A("x64", 4 * a + t, 4 * b, 4), ALU.add)
-                scaled(A(xn, 4 * a + t, 4 * b, 4), A("tmp", 448 * t + a, 448 * t + b), 2.0 ** -6)
+        for c in range(1, len(CHZ)):
+            finish(c)
 
-    for c, (a, b) in enumerate(CH):
+    for c, (a, b) in enumerate(CHX):
         quant(A("qx3", a, b), A("qxs3", a, b), A("x3", 4 * a, 4 * b))
         mm(A("pa", 512 * c, 512 * c + b - a), A("qv"), A("qvs"), A("qx3", a, b), A("qxs3", a, b))
     copy(A("p7"), A("wb", 0, 448, by=A("vr3")), "s")
     dma("y", ext(T.pl[0:7, :]), (T.p7[16:128:16, :], A("p7")[1]), "op_")
     copy(A("p8"), A("wb", 0, 448, by=A("r8")), "s")
     dma("y", ext(T.pl[7:8, :]), A("p8", p=(112, 113)), "op_")
-    for c, (a, b) in enumerate(CH):
-        copy(A("yb", a, b), A("pa", 512 * c, 512 * c + b - a))
+    for c, (a, b) in enumerate(CHX):
         dma("y", ext(T.oc[:, 4 * a:4 * b]), A("qx3", a, b, cast=dt.uint8), "oo")
+        copy(A("yb", a, b), A("pa", 512 * c, 512 * c + b - a), "vs"[c])
         dma("y" if c else "s", ext(T.y[:, a:b]), A("yb", a, b), "oy")
     for i in range(4):
         dma("s", ext(T.osc[4 * i:4 * i + 4, :]), A("qxs3", p=(32 * i, 32 * i + 4)), "os_")

@@ -4,8 +4,9 @@ from concourse.mybir import dt, AluOpType, ActivationFunctionType
 C = 448
 STEPS = (1, 2, 3)
 CHH = ((0, 224), (224, 448))
-CHZ = ((0, 128), (128, 288), (288, 448))
-CHX = ((0, 288), (288, 448))
+CHZ = ((0, 160), (160, 320), (320, 448))
+CHX = ((0, 320), (320, 448))
+PIECE = 112
 BIG = 524288.0
 ALU = AluOpType
 COPY = ActivationFunctionType.Copy
@@ -27,7 +28,7 @@ SCRATCH = {
     "hi": ("sbuf", [128, 1], I32), "off": ("sbuf", [128, 1], F32),
     "m16": ("sbuf", [128, 16], F32), "da": ("sbuf", [128, 16], F32), "db": ("sbuf", [128, 16], F32),
     "dc": ("sbuf", [128, 16], F32), "dd": ("sbuf", [128, 16], F32), "de": ("sbuf", [128, 16], F32),
-    "d": ("sbuf", [128, 448], F32), "idl": ("sbuf", [128, 28], I32), "pat": ("sbuf", [128, 896], F32),
+    "d": ("sbuf", [128, 448], F32), "idl": ("sbuf", [128, 28], I32), "pat": ("sbuf", [128, 448], F32),
     "wb": ("sbuf", [128, 1792], F32),
     "b1": ("sbuf", [128, 448], F32), "b2": ("sbuf", [128, 448], F32), "t2": ("sbuf", [128, 448], F32),
     "t1": ("sbuf", [128, 448], I32), "n1": ("sbuf", [128, 448], I32),
@@ -35,8 +36,8 @@ SCRATCH = {
     "o5": ("sbuf", [128, 448], F32), "s5": ("sbuf", [128, 448], F32),
     "i2": ("sbuf", [128, 28], I32), "j2": ("sbuf", [128, 28], I32), "l1": ("sbuf", [128, 28], U16),
     "l2": ("sbuf", [128, 28], U16), "l3": ("sbuf", [128, 28], U16),
-    "nat": ("sbuf", [128, 896], F32), "nsc": ("sbuf", [128, 448], F32),
-    "natb": ("sbuf", [128, 896], F32), "nscb": ("sbuf", [128, 448], F32),
+    "na0": ("sbuf", [128, 896], F32), "nb0": ("sbuf", [128, 896], F32),
+    "na1": ("sbuf", [128, 896], F32), "nb1": ("sbuf", [128, 896], F32),
     "tmp": ("sbuf", [128, 1792], F32), "x64": ("sbuf", [128, 1792], BF),
     "o8": ("sbuf", [128, 448], F32), "s8": ("sbuf", [128, 448], F32), "l8": ("sbuf", [128, 28], U16), "r8": ("sbuf", [128, 28], U16),
     "p7": ("sbuf", [128, 448], F32), "p8": ("sbuf", [128, 448], F32), "yb": ("sbuf", [128, 448], F32),
@@ -208,6 +209,13 @@ def rank_program(g, core, T, topo):
     def bank(c, t, n):
         return A(("pa", "pb")[c % 2], 512 * t, 512 * t + n)
 
+    spare = []
+
+    def gap(n=1):
+        while n and spare:
+            spare.pop(0)()
+            n -= 1
+
     dma("y", A("gli"), ext(T.gl[:, :]), "dgl")
     dma("s", A("hti"), ext(T.ht[:, :]), "dht")
     for k, (a, b) in enumerate(CHX):
@@ -217,75 +225,104 @@ def rank_program(g, core, T, topo):
     dma("y", A("qw", cast=dt.uint8), ext(T.wc[:, :]), "dw")
     dma("y", A("vt"), ext(T.v[:, :]), "dv")
 
-    fill(A("wt"), 0.0)
+    for k in range(4):
+        spare.append(lambda k=k: fill(A("ec", 512 * k, 512 * k + 512), 1.0))
+    for k in range(2):
+        spare.append(lambda k=k: fill(A("pat", k, 448, 2), (1024.0, 1.0)[k]))
     iota(A("m16"), [[1, 16]], 0, 0, True)
     iota(A("pi"), [[0, 1]], 0, 1)
     iota(A("uli"), [[16, 2], [32, 4], [0, 2]], 0, 0)
     iota(A("idl"), [[16, 28]], 0, 1)
     iota(A("wb", 0, 448), [[1, 448]], 0, 0, True)
+    fill(A("wt"), 0.0)
+    fill(A("l2"), 0)
+    gap(2)
     ts(A("lo"), A("pi"), 15, ALU.bitwise_and)
     ts(A("hi"), A("pi"), 4, ALU.logical_shift_right, 1, ALU.bitwise_and)
     ts(A("dc"), A("m16"), 15.0, ALU.is_equal, -2.0, ALU.mult)
+    copy(A("ul"), A("uli"))
     copy(A("lof"), A("lo"))
     ts(A("off"), A("hi"), 448.0, ALU.mult, BIG, ALU.add)
-    copy(A("ul"), A("uli"))
+    gap()
     ts(A("da"), A("m16"), A("lof"), ALU.is_ge)
     ts(A("db"), A("m16"), A("lof"), ALU.is_equal)
-    fill(A("l2"), 0)
+    gap()
     tt(A("dd"), A("da"), A("db"), ALU.add)
+    gap()
     tt(A("de"), A("dd"), A("dc"), ALU.add)
+    gap()
     ts(A("d", 0, 16), A("de"), -1.0, ALU.add, BIG, ALU.mult)
-    w = 16
-    while w < C:
-        n = min(w, C - w)
-        copy(A("d", w, w + n), A("d", 0, n))
-        w += n
     copy(A("wt", 0, 56), A("gli"))
+    w = [16]
+
+    def widen():
+        if w[0] < C:
+            n = min(w[0], C - w[0])
+            copy(A("d", w[0], w[0] + n), A("d", 0, n))
+            w[0] += n
+
+    widen()
     turn(A("tg", 0, 64), A("wt", 0, 64))
     turn(A("tg", 64, 128), A("wt", 0, 64))
+    widen()
     for k in (0, 32):
         copy(A("tg", k + 16, k + 32), A("tg", k, k + 16))
         copy(A("tg", 64 + k, 64 + k + 16), A("tg", 64 + k + 16, 64 + k + 32))
+    widen()
     turn(A("tg2"), A("tg"))
+    widen()
     copy(A("gs", 0, 56), A("tg2", 0, 56))
     copy(A("gs", 56, 112), A("tg2", 64, 120))
     send(1, A("gr1"), A("gs"), "g1")
+    send_both()
     for s in STEPS:
         arrives(s, A("gr%d" % s), "g%d" % s, 1 if s == 1 else 2)
+    run("p", lambda: g.affine_select(T.ec[:, :], T.ec[:, :], [[1, 4], [-1, 512]], ALU.is_equal, 0.0, 0, 4), [A("ec")], [A("ec")])
+    copy(A("wt", 64, 92), A("hti"))
     for t in range(4):
         ts(A("hl", 28 * t, 28 * t + 28), A("hti"), 4.0, ALU.mult, float(t), ALU.add)
-    fill(A("ec"), 1.0)
-    run("p", lambda: g.affine_select(T.ec[:, :], T.ec[:, :], [[1, 4], [-1, 512]], ALU.is_equal, 0.0, 0, 4), [A("ec")], [A("ec")])
+    turn(A("th", 0, 32), A("wt", 64, 96))
+    turn(A("th", 32, 64), A("wt", 64, 96))
+    widen()
+    copy(A("th", 16, 32), A("th", 0, 16))
+    copy(A("th", 32, 48), A("th", 48, 64))
     quant(A("qu"), A("qus"), A("ut"))
+    turn(A("th2"), A("th"))
     ul = A("ul")
     copy(A("qps"), A("qus", by=ul), "s")
     copy(A("qp", cast=dt.uint32), A("qu", cast=dt.uint32, by=ul))
-    copy(A("wt", 64, 92), A("hti"))
-    turn(A("th", 0, 32), A("wt", 64, 96))
-    turn(A("th", 32, 64), A("wt", 64, 96))
-    copy(A("th", 16, 32), A("th", 0, 16))
-    copy(A("th", 32, 48), A("th", 48, 64))
-    turn(A("th2"), A("th"))
     copy(A("hx", 0, 28), A("th2", 0, 28))
     copy(A("hx", 28, 56), A("th2", 32, 60))
 
-    def table(s, wave, fused):
-        lst = A("gr%d" % s, 56 * wave, 56 * wave + 56)
-        e = "%s%d" % (("ea", "eb")[wave], s)
-        nat, nsc = (("nat", "nsc"), ("natb", "nscb"))[wave]
-        if fused:
-            tt(A(nat), A("wb", 0, 448, by=lst), A("pat"), ALU.mult)
-            return lambda a=0, b=C: tt(A(e, a, b), A(nat, 2 * a, 2 * b, 2), A(nat, 2 * a + 1, 2 * b, 2), ALU.add)
-        copy(A(nat), A("wb", 0, 448, by=lst), "s")
-        scaled(A(nsc), A(nat, 0, 896, 2), 1024.0)
-        return lambda a=0, b=C: tt(A(e, a, b), A(nsc, a, b), A(nat, 2 * a + 1, 2 * b, 2), ALU.add)
+    def nature(s, wave):
+        nat = ("na%d", "nb%d")[wave] % (s % 2)
+        lst = 56 * wave
+        if s == 1 and wave == 0:
+            tt(A(nat, 0, 448), A("wb", 0, 448, by=A("gr1", 0, 28)), A("pat"), ALU.mult)
+            copy(A(nat, 448, 896), A("wb", 0, 448, by=A("gr1", 28, 56)), "s")
+            scaled(A(nat, 448, 896, 2), A(nat, 448, 896, 2), 1024.0)
+        else:
+            copy(A(nat), A("wb", 0, 448, by=A("gr%d" % s, lst, lst + 56)), "s")
+            scaled(A(nat, 0, 896, 2), A(nat, 0, 896, 2), 1024.0)
 
-    early = late = None
+    def join(s, wave, a, b):
+        nat = ("na%d", "nb%d")[wave] % (s % 2)
+        tt(A(("ea%d", "eb%d")[wave] % s, a, b), A(nat, 2 * a, 2 * b, 2), A(nat, 2 * a + 1, 2 * b, 2), ALU.add)
+
     for s in STEPS:
         k = "%d" % s
         xo, xn = "x%d" % (s - 1), "x" + k
         qx, qxs = "qx%d" % (s - 1), "qxs%d" % (s - 1)
         first = s == 1
+        if s < 3:
+            for wave in range(2):
+                for a in range(0, C, PIECE):
+                    spare.append(lambda wave=wave, a=a: join(s + 1, wave, a, a + PIECE))
+
+        def host_gather(c):
+            a, b = CHH[c]
+            for t in range(4):
+                copy(A("h" + k, 4 * a + t, 4 * b, 4), A(xo, by=A("hl", 28 * t + a // 16, 28 * t + b // 16)), "s")
 
         def host_send(c):
             a, b = CHH[c]
@@ -304,61 +341,69 @@ def rank_program(g, core, T, topo):
         for c, (a, b) in enumerate(CHX):
             quant(A(qx, a, b), A(qxs, a, b), A(xo, 4 * a, 4 * b))
             if not first:
-                late(224 * c, 224 * c + 224)
+                gap()
         for n in range(2):
             for c, (a, b) in enumerate(CHX):
                 w = 512 * (2 * n + c)
                 mm(A("pa", w, w + b - a), A("qp", 128 * n, 128 * n + 128), A("qps", 128 * n, 128 * n + 128), A(qx, a, b), A(qxs, a, b))
-        for a, b in CHH:
-            for t in range(4):
-                copy(A("h" + k, 4 * a + t, 4 * b, 4), A(xo, by=A("hl", 28 * t + a // 16, 28 * t + b // 16)), "s")
+        host_gather(0)
+        if first:
+            nature(1, 0)
+            nature(1, 1)
+        host_gather(1)
         bits(0, 0)
         bits(0, 1)
         if first:
-            late = table(1, 1, False)
+            join(1, 0, 0, 224)
+            join(1, 0, 224, 448)
             bits(1, 0)
-            bits(1, 1)
-            fill(A("pat", 0, 896, 2), 1024.0)
-            fill(A("pat", 1, 896, 2), 1.0)
-            host_send(0)
-            table(1, 0, True)()
         tt(A("t2"), A("b2", by=A("hx", 0, 28)), A("ea" + k), ALU.mult)
-        if not first:
-            bits(1, 0)
+        bits(1, 1 if first else 0)
         scan(A("s2"), A("t2"))
         if first:
-            host_send(1)
-            send_both()
+            host_send(0)
         else:
             bits(1, 1)
         copy(A("i2"), wrapped("s2"))
         if first:
-            late()
+            join(1, 1, 0, 448)
         else:
             host_send(0)
         ts(A("j2"), A("i2"), 1023, ALU.bitwise_and)
         tt(A("t1"), A("b1", by=A("hx", 28, 56)), A("eb" + k), ALU.mult)
         copy(A("l1"), A("j2"))
-        ts(A("n1"), A("t1"), 1023, ALU.bitwise_and)
+        if first:
+            nature(2, 0)
+            nature(2, 1)
         copy(A("wb", 448, 896), A("wb", 0, 448, by=A("l1")), "s")
-        if not first:
-            host_send(1)
+        host_send(1)
+        ts(A("n1"), A("t1"), 1023, ALU.bitwise_and)
         scaled(A("x64"), A(xo), 64.0)
-        if s < 3:
-            early, late = table(s + 1, 0, False), table(s + 1, 1, False)
-        copy(A("wb", 896, 1344), A("n1", by=A("l1")))
+        if first:
+            nature(3, 0)
+            nature(3, 1)
         copy(A("l3", p=(0, 32)), A("j2", p=(0, 32)))
-        scan(A("s3"), A("wb", 896, 1344))
+        gap()
+        copy(A("wb", 896, 1344), A("n1", by=A("l1")))
         copy(A("l3", p=(0, 16)), A("idl", p=(0, 16)))
+        gap()
+        scan(A("s3"), A("wb", 896, 1344))
+        gap()
         ts(A("l2", p=(32, 64)), wrapped("s3", (0, 32)), BIG + 896.0, ALU.add)
         ts(A("l2", p=(96, 128)), wrapped("s3", (64, 96)), A("off", p=(64, 96)), ALU.add)
         ts(A("l3", p=(32, 64)), wrapped("s3", (0, 32)), A("off", p=(0, 32)), ALU.add)
+        gap()
         copy(A("wb", 1344, 1792), A("wb", 0, 1344, by=A("l2")))
+        gap()
         scan(A("s4"), A("wb", 1344, 1792))
+        gap()
         ts(A("l3", p=(64, 96)), wrapped("s4", (32, 64)), A("off", p=(32, 64)), ALU.add)
         ts(A("l3", p=(96, 128)), wrapped("s4", (32, 64)), BIG + 1344.0, ALU.add)
+        gap()
         copy(A("o5"), A("wb", by=A("l3")))
+        gap()
         scan(A("s5"), A("o5"))
+        gap()
         ts(A("vl" + k), wrapped("s5"), BIG, ALU.add)
         send(s, A("vr" + k), A("vl" + k), "k" + k)
         arrives(s, A("vr" + k), "k" + k)
@@ -371,45 +416,60 @@ def rank_program(g, core, T, topo):
         if first:
             quant(A("qe"), A("qes"), A("ec"))
             quant(A("qv"), A("qvs"), A("vt"))
-        if s < 3:
-            early()
+        gap(len(spare))
         for c, (a, b) in enumerate(CHH):
             for t in range(4):
                 mm(bank(c, t, b - a), A("qe", 128 * t, 128 * t + 128), A("qes", 128 * t, 128 * t + 128), A("hc" + k, a, b), A("hcs" + k, a, b))
             for t in range(4):
                 tt(A("m" + k, 448 * t + a, 448 * t + b), A(xo, 4 * a + t, 4 * b, 4), bank(c, t, b - a), ALU.max)
+
+        def mosaic(c, t):
+            a, b = CHZ[c]
+            copy(A("z" + k, 4 * a + t, 4 * b, 4), A("m" + k, 448 * t, 448 * t + 448, by=A("vr" + k, a // 16, b // 16)), "v" if t < 2 else "s")
+
+        def layer(c):
+            a, b = CHZ[c]
+            quant(A("qz" + k, a, b), A("qzs" + k, a, b), A("z" + k, 4 * a, 4 * b))
+            for t in range(4):
+                mm(bank(c, t, b - a), A("qw", 128 * t, 128 * t + 128), A("qws", 128 * t, 128 * t + 128),
+                   A("qz" + k, a, b), A("qzs" + k, a, b))
+
         def finish(c):
             a, b = CHZ[c]
             for t in range(4):
                 tt(A("tmp", 448 * t + a, 448 * t + b), bank(c, t, b - a), A("x64", 4 * a + t, 4 * b, 4), ALU.add)
                 scaled(A(xn, 4 * a + t, 4 * b, 4), A("tmp", 448 * t + a, 448 * t + b), 2.0 ** -6)
 
-        for c, (a, b) in enumerate(CHZ):
-            by = A("vr" + k, a // 16, b // 16)
-            for t in (0, 2, 1, 3):
-                copy(A("z" + k, 4 * a + t, 4 * b, 4), A("m" + k, 448 * t, 448 * t + 448, by=by), "v" if t < 2 else "s")
-            quant(A("qz" + k, a, b), A("qzs" + k, a, b), A("z" + k, 4 * a, 4 * b))
-            if c == 2:
-                finish(0)
-            for t in range(4):
-                mm(bank(c, t, b - a), A("qw", 128 * t, 128 * t + 128), A("qws", 128 * t, 128 * t + 128),
-                   A("qz" + k, a, b), A("qzs" + k, a, b))
-        for c in range(1, len(CHZ)):
-            finish(c)
+        for c in range(3):
+            mosaic(c, 2)
+            mosaic(c, 3)
+        if s == 3:
+            copy(A("p7"), A("wb", 0, 448, by=A("vr3")), "s")
+            dma("y", ext(T.pl[0:7, :]), (T.p7[16:128:16, :], A("p7")[1]), "op_")
+        mosaic(0, 0)
+        mosaic(0, 1)
+        mosaic(1, 0)
+        layer(0)
+        mosaic(1, 1)
+        mosaic(2, 0)
+        layer(1)
+        mosaic(2, 1)
+        finish(0)
+        layer(2)
+        finish(1)
+        finish(2)
 
     for c, (a, b) in enumerate(CHX):
         quant(A("qx3", a, b), A("qxs3", a, b), A("x3", 4 * a, 4 * b))
         mm(A("pa", 512 * c, 512 * c + b - a), A("qv"), A("qvs"), A("qx3", a, b), A("qxs3", a, b))
-    copy(A("p7"), A("wb", 0, 448, by=A("vr3")), "s")
-    dma("y", ext(T.pl[0:7, :]), (T.p7[16:128:16, :], A("p7")[1]), "op_")
-    copy(A("p8"), A("wb", 0, 448, by=A("r8")), "s")
-    dma("y", ext(T.pl[7:8, :]), A("p8", p=(112, 113)), "op_")
-    for c, (a, b) in enumerate(CHX):
         dma("y", ext(T.oc[:, 4 * a:4 * b]), A("qx3", a, b, cast=dt.uint8), "oo")
-        copy(A("yb", a, b), A("pa", 512 * c, 512 * c + b - a), "vs"[c])
-        dma("y" if c else "s", ext(T.y[:, a:b]), A("yb", a, b), "oy")
+    copy(A("p8"), A("wb", 0, 448, by=A("r8")), "s")
     for i in range(4):
         dma("s", ext(T.osc[4 * i:4 * i + 4, :]), A("qxs3", p=(32 * i, 32 * i + 4)), "os_")
+    dma("s", ext(T.pl[7:8, :]), A("p8", p=(112, 113)), "op_")
+    for c, (a, b) in enumerate(CHX):
+        copy(A("yb", a, b), A("pa", 512 * c, 512 * c + b - a))
+        dma("y", ext(T.y[:, a:b]), A("yb", a, b), "oy")
     for sem in sorted(total):
         if seen["p"].get(sem, 0) < total[sem]:
             g.wait_ge(T.sem[sem], total[sem])

@@ -5,61 +5,38 @@ C = 448
 STEPS = (1, 2, 3)
 CHH = ((0, 224), (224, 448))
 CHZ = ((0, 160), (160, 320), (320, 448))
-CHX = ((0, 320), (320, 448))
+CHL = ((0, 320), (320, 448))
 PIECE = 112
 BIG = 524288.0
 ALU = AluOpType
 COPY = ActivationFunctionType.Copy
 F8, U8, BF, F32, I32, U16 = "float8_e4m3fn_x4", "uint8", "bfloat16", "float32", "int32", "uint16"
 
-SCRATCH = {
-    "gli": ("sbuf", [128, 56], I32), "hti": ("sbuf", [128, 28], I32),
-    "wt": ("sbuf", [128, 96], F32), "tg": ("sbuf", [128, 128], F32), "tg2": ("sbuf", [128, 128], F32),
-    "th": ("sbuf", [128, 64], F32), "th2": ("sbuf", [128, 64], F32),
-    "gs": ("sbuf", [128, 112], U16), "hx": ("sbuf", [128, 56], U16), "hl": ("sbuf", [128, 112], U16),
-    "ut": ("sbuf", [128, 512], BF), "vt": ("sbuf", [128, 512], BF), "ec": ("sbuf", [128, 2048], BF),
-    "qu": ("sbuf", [128, 128], F8), "qus": ("sbuf", [128, 128], U8),
-    "qp": ("sbuf", [128, 256], F8), "qps": ("sbuf", [128, 256], U8),
-    "qv": ("sbuf", [128, 128], F8), "qvs": ("sbuf", [128, 128], U8),
-    "qe": ("sbuf", [128, 512], F8), "qes": ("sbuf", [128, 512], U8),
-    "qw": ("sbuf", [128, 512], F8), "qws": ("sbuf", [128, 512], U8),
-    "uli": ("sbuf", [128, 16], I32), "ul": ("sbuf", [128, 16], U16),
-    "pi": ("sbuf", [128, 1], I32), "lo": ("sbuf", [128, 1], I32), "lof": ("sbuf", [128, 1], F32),
-    "hi": ("sbuf", [128, 1], I32), "off": ("sbuf", [128, 1], F32),
-    "m16": ("sbuf", [128, 16], F32), "da": ("sbuf", [128, 16], F32), "db": ("sbuf", [128, 16], F32),
-    "dc": ("sbuf", [128, 16], F32), "dd": ("sbuf", [128, 16], F32), "de": ("sbuf", [128, 16], F32),
-    "d": ("sbuf", [128, 448], F32), "idl": ("sbuf", [128, 28], I32), "pat": ("sbuf", [128, 448], F32),
-    "wb": ("sbuf", [128, 1792], F32),
-    "b1": ("sbuf", [128, 448], F32), "b2": ("sbuf", [128, 448], F32), "t2": ("sbuf", [128, 448], F32),
-    "t1": ("sbuf", [128, 448], I32), "n1": ("sbuf", [128, 448], I32),
-    "s2": ("sbuf", [128, 448], F32), "s3": ("sbuf", [128, 448], F32), "s4": ("sbuf", [128, 448], F32),
-    "o5": ("sbuf", [128, 448], F32), "s5": ("sbuf", [128, 448], F32),
-    "i2": ("sbuf", [128, 28], I32), "j2": ("sbuf", [128, 28], I32), "l1": ("sbuf", [128, 28], U16),
-    "l2": ("sbuf", [128, 28], U16), "l3": ("sbuf", [128, 28], U16),
-    "na0": ("sbuf", [128, 896], F32), "nb0": ("sbuf", [128, 896], F32),
-    "na1": ("sbuf", [128, 896], F32), "nb1": ("sbuf", [128, 896], F32),
-    "tmp": ("sbuf", [128, 1792], F32), "x64": ("sbuf", [128, 1792], BF),
-    "o8": ("sbuf", [128, 448], F32), "s8": ("sbuf", [128, 448], F32), "l8": ("sbuf", [128, 28], U16), "r8": ("sbuf", [128, 28], U16),
-    "p7": ("sbuf", [128, 448], F32), "p8": ("sbuf", [128, 448], F32), "yb": ("sbuf", [128, 448], F32),
-    "pa": ("psum", [128, 2048], F32), "pb": ("psum", [128, 2048], F32),
-}
+SCRATCH = {"pa": ("psum", [128, 2048], F32), "pb": ("psum", [128, 2048], F32)}
+
+
+def _sbuf(kind, **widths):
+    for name in widths:
+        SCRATCH[name] = ("sbuf", [128, widths[name]], kind)
+
+
+_sbuf(I32, gli=56, hti=28, uli=16, pi=1, lo=1, hi=1, idl=28, t1=448, n1=448)
+_sbuf(U16, gs=112, hx=56, hl=112, ul=16, l1=28, l2=28, l3=28, l8=28, r8=28)
+_sbuf(BF, ut=512, vt=512, ec=2048, eye=128, x64=1792)
+_sbuf(F8, qu=128, qp=256, qv=128, qe=512, qw=512)
+_sbuf(U8, qus=128, qps=256, qvs=128, qes=512, qws=512)
+_sbuf(F32, wt=96, tg=128, tg2=128, th=64, th2=64, lof=1, off=1, m16=16, da=16, db=16, dc=16, dd=16, de=16, d=448, gw=448,
+      wb=1792, b1=448, b2=448, t2=448, s2=448, s3=448, s4=448, o5=448, s5=448, lf=28, na0=896, nb0=896, na1=896, nb1=896,
+      tmp=1792, o8=448, s8=448, p7=448, p8=448, yb=448)
 for _k in range(4):
     SCRATCH["x%d" % _k] = ("sbuf", [128, 1792], BF)
     SCRATCH["qx%d" % _k] = ("sbuf", [128, 448], F8)
     SCRATCH["qxs%d" % _k] = ("sbuf", [128, 448], U8)
 for _k in STEPS:
-    SCRATCH["h%d" % _k] = ("sbuf", [128, 1792], BF)
-    SCRATCH["m%d" % _k] = ("sbuf", [128, 1792], BF)
-    SCRATCH["z%d" % _k] = ("sbuf", [128, 1792], BF)
-    for _n in ("qh", "hc", "qz"):
-        SCRATCH["%s%d" % (_n, _k)] = ("sbuf", [128, 448], F8)
-    for _n in ("qhs", "hcs", "qzs"):
-        SCRATCH["%s%d" % (_n, _k)] = ("sbuf", [128, 448], U8)
-    for _n in ("vl", "vr"):
-        SCRATCH["%s%d" % (_n, _k)] = ("sbuf", [128, 28], U16)
-    SCRATCH["gr%d" % _k] = ("sbuf", [128, 112], U16)
-    for _n in ("ea", "eb"):
-        SCRATCH["%s%d" % (_n, _k)] = ("sbuf", [128, 448], F32)
+    for _n, _w, _d in (("h", 1792, BF), ("m", 1792, BF), ("z", 1792, BF), ("qh", 448, F8), ("hc", 448, F8), ("qz", 448, F8),
+                       ("qhs", 448, U8), ("hcs", 448, U8), ("qzs", 448, U8), ("vl", 28, U16), ("vr", 28, U16), ("gr", 112, U16),
+                       ("ea", 448, F32), ("eb", 448, F32)):
+        SCRATCH["%s%d" % (_n, _k)] = ("sbuf", [128, _w], _d)
 SEMAPHORES = ["v", "s", "t", "p", "rl", "k8", "dgl", "dht", "dx0", "dx1", "du", "dw", "dv", "oo", "os_", "oy", "op_"]
 for _k in STEPS:
     SEMAPHORES += ["g%d" % _k, "k%d" % _k, "c%da" % _k, "c%db" % _k]
@@ -209,6 +186,9 @@ def rank_program(g, core, T, topo):
     def bank(c, t, n):
         return A(("pa", "pb")[c % 2], 512 * t, 512 * t + n)
 
+    def score(i, n):
+        return A(("pb", "pa")[i // 4], 512 * (i % 4), 512 * (i % 4) + n)
+
     spare = []
 
     def gap(n=1):
@@ -218,20 +198,21 @@ def rank_program(g, core, T, topo):
 
     dma("y", A("gli"), ext(T.gl[:, :]), "dgl")
     dma("s", A("hti"), ext(T.ht[:, :]), "dht")
-    for k, (a, b) in enumerate(CHX):
+    for k, (a, b) in enumerate(CHL):
         dma("s" if k == 0 else "y", A("x0", 4 * a, 4 * b), ext(T.x[:, 4 * a:4 * b]), "dx%d" % k)
     dma("y", A("ut"), ext(T.u[:, :]), "du")
+    waits("y", A("x0")[1] + A("ut")[1], [])
     dma("y", A("qws"), ext(T.ws[:, :]), "dw")
     dma("y", A("qw", cast=dt.uint8), ext(T.wc[:, :]), "dw")
     dma("y", A("vt"), ext(T.v[:, :]), "dv")
 
     for k in range(4):
-        spare.append(lambda k=k: fill(A("ec", 512 * k, 512 * k + 512), 1.0))
-    for k in range(2):
-        spare.append(lambda k=k: fill(A("pat", k, 448, 2), (1024.0, 1.0)[k]))
+        spare.append(lambda k=k: fill(A("ec", 512 * k, 512 * k + 512), 0.0))
+    fill(A("eye"), 1.0)
     iota(A("m16"), [[1, 16]], 0, 0, True)
     iota(A("pi"), [[0, 1]], 0, 1)
     iota(A("uli"), [[16, 2], [32, 4], [0, 2]], 0, 0)
+    run("p", lambda: g.affine_select(T.eye[:, :], T.eye[:, :], [[-1, 128]], ALU.is_equal, 0.0, 0, 1), [A("eye")], [A("eye")])
     iota(A("idl"), [[16, 28]], 0, 1)
     iota(A("wb", 0, 448), [[1, 448]], 0, 0, True)
     fill(A("wt"), 0.0)
@@ -248,11 +229,13 @@ def rank_program(g, core, T, topo):
     ts(A("db"), A("m16"), A("lof"), ALU.is_equal)
     gap()
     tt(A("dd"), A("da"), A("db"), ALU.add)
-    gap()
-    tt(A("de"), A("dd"), A("dc"), ALU.add)
-    gap()
-    ts(A("d", 0, 16), A("de"), -1.0, ALU.add, BIG, ALU.mult)
+    for t in range(4):
+        copy(A("ec", 513 * t, 512 * t + 512, 4), A("eye"), "s")
     copy(A("wt", 0, 56), A("gli"))
+    tt(A("de"), A("dd"), A("dc"), ALU.add)
+    turn(A("tg", 0, 64), A("wt", 0, 64))
+    turn(A("tg", 64, 128), A("wt", 0, 64))
+    ts(A("d", 0, 16), A("de"), -1.0, ALU.add, BIG, ALU.mult)
     w = [16]
 
     def widen():
@@ -261,10 +244,6 @@ def rank_program(g, core, T, topo):
             copy(A("d", w[0], w[0] + n), A("d", 0, n))
             w[0] += n
 
-    widen()
-    turn(A("tg", 0, 64), A("wt", 0, 64))
-    turn(A("tg", 64, 128), A("wt", 0, 64))
-    widen()
     for k in (0, 32):
         copy(A("tg", k + 16, k + 32), A("tg", k, k + 16))
         copy(A("tg", 64 + k, 64 + k + 16), A("tg", 64 + k + 16, 64 + k + 32))
@@ -277,51 +256,75 @@ def rank_program(g, core, T, topo):
     send_both()
     for s in STEPS:
         arrives(s, A("gr%d" % s), "g%d" % s, 1 if s == 1 else 2)
-    run("p", lambda: g.affine_select(T.ec[:, :], T.ec[:, :], [[1, 4], [-1, 512]], ALU.is_equal, 0.0, 0, 4), [A("ec")], [A("ec")])
     copy(A("wt", 64, 92), A("hti"))
     for t in range(4):
         ts(A("hl", 28 * t, 28 * t + 28), A("hti"), 4.0, ALU.mult, float(t), ALU.add)
     turn(A("th", 0, 32), A("wt", 64, 96))
     turn(A("th", 32, 64), A("wt", 64, 96))
     widen()
+    widen()
     copy(A("th", 16, 32), A("th", 0, 16))
     copy(A("th", 32, 48), A("th", 48, 64))
-    quant(A("qu"), A("qus"), A("ut"))
+    widen()
     turn(A("th2"), A("th"))
+    quant(A("qe"), A("qes"), A("ec"))
+    copy(A("hx", 0, 28), A("th2", 0, 28))
+    copy(A("hx", 28, 56), A("th2", 32, 60))
+    quant(A("qu"), A("qus"), A("ut"))
     ul = A("ul")
     copy(A("qps"), A("qus", by=ul), "s")
     copy(A("qp", cast=dt.uint32), A("qu", cast=dt.uint32, by=ul))
-    copy(A("hx", 0, 28), A("th2", 0, 28))
-    copy(A("hx", 28, 56), A("th2", 32, 60))
 
     def nature(s, wave):
         nat = ("na%d", "nb%d")[wave] % (s % 2)
         lst = 56 * wave
         if s == 1 and wave == 0:
-            tt(A(nat, 0, 448), A("wb", 0, 448, by=A("gr1", 0, 28)), A("pat"), ALU.mult)
+            copy(A(nat, 0, 448), A("wb", 0, 448, by=A("gr1", 0, 28)))
             copy(A(nat, 448, 896), A("wb", 0, 448, by=A("gr1", 28, 56)), "s")
-            scaled(A(nat, 448, 896, 2), A(nat, 448, 896, 2), 1024.0)
         else:
             copy(A(nat), A("wb", 0, 448, by=A("gr%d" % s, lst, lst + 56)), "s")
+        if wave:
             scaled(A(nat, 0, 896, 2), A(nat, 0, 896, 2), 1024.0)
 
     def join(s, wave, a, b):
         nat = ("na%d", "nb%d")[wave] % (s % 2)
-        tt(A(("ea%d", "eb%d")[wave] % s, a, b), A(nat, 2 * a, 2 * b, 2), A(nat, 2 * a + 1, 2 * b, 2), ALU.add)
+        tt(A(("ea%d", "eb%d")[wave] % s, a, b), A(nat, 2 * a + 1, 2 * b, 2), A(nat, 2 * a, 2 * b, 2), (ALU.subtract, ALU.add)[wave])
 
+    def even(s):
+        scan(A("gw"), A("na%d" % (s % 2), 0, 896, 2))
+
+    def halves(out, a, b, name):
+        copy(A(out, a, a + 224), A("wb", 0, b, by=A(name, 0, 14)))
+        copy(A(out, a + 224, a + 448), A("wb", 0, b, by=A(name, 14, 28)), "s")
+
+    def settle(s, c):
+        a, b = CHZ[c]
+        q, sc = A("qx%d" % s, a, b), A("qxs%d" % s, a, b)
+        quant(q, sc, A("x%d" % s, 4 * a, 4 * b))
+        if s < 3:
+            mm(score(c, b - a), A("qp", 0, 128), A("qps", 0, 128), q, sc)
+        else:
+            mm(score(c, b - a), A("qv"), A("qvs"), q, sc)
+            if c:
+                a, b = CHL[c - 1]
+                dma("y", ext(T.oc[:, 4 * a:4 * b]), A("qx3", a, b, cast=dt.uint8), "oo")
+
+    for c in range(3):
+        settle(0, c)
     for s in STEPS:
         k = "%d" % s
         xo, xn = "x%d" % (s - 1), "x" + k
         qx, qxs = "qx%d" % (s - 1), "qxs%d" % (s - 1)
         first = s == 1
+        for a in range(0, 1792, 448):
+            spare.append(lambda a=a: ts(A("x64", a, a + 448), A(xo, a, a + 448), 64.0, ALU.mult))
         if s < 3:
-            for wave in range(2):
-                for a in range(0, C, PIECE):
-                    spare.append(lambda wave=wave, a=a: join(s + 1, wave, a, a + PIECE))
+            for a in range(0, C, PIECE):
+                spare.append(lambda a=a: join(s + 1, 0, a, a + PIECE))
 
-        def host_gather(c):
+        def host_gather(c, which):
             a, b = CHH[c]
-            for t in range(4):
+            for t in which:
                 copy(A("h" + k, 4 * a + t, 4 * b, 4), A(xo, by=A("hl", 28 * t + a // 16, 28 * t + b // 16)), "s")
 
         def host_send(c):
@@ -334,55 +337,57 @@ def rank_program(g, core, T, topo):
             arrives(s, A("hcs" + k, a, b), sem)
 
         def bits(n, c):
-            a, b = CHX[c]
-            w = 512 * (2 * n + c)
-            ts(A(("b2", "b1")[n], a, b), A("pa", w, w + b - a), 0.0, ALU.is_gt, 2.0 ** -10, ALU.max)
+            a, b = CHZ[c]
+            if n == 0:
+                ts(A("b2", a, b), score(c, b - a), 0.0, ALU.is_gt)
+            else:
+                ts(A("b1", a, b), score(3 + c, b - a), 0.0, ALU.is_gt, 2.0 ** -10, ALU.max)
 
-        for c, (a, b) in enumerate(CHX):
-            quant(A(qx, a, b), A(qxs, a, b), A(xo, 4 * a, 4 * b))
-            if not first:
-                gap()
-        for n in range(2):
-            for c, (a, b) in enumerate(CHX):
-                w = 512 * (2 * n + c)
-                mm(A("pa", w, w + b - a), A("qp", 128 * n, 128 * n + 128), A("qps", 128 * n, 128 * n + 128), A(qx, a, b), A(qxs, a, b))
-        host_gather(0)
+        for c, (a, b) in enumerate(CHZ):
+            mm(score(3 + c, b - a), A("qp", 128, 256), A("qps", 128, 256), A(qx, a, b), A(qxs, a, b))
         if first:
+            host_gather(0, (0,))
             nature(1, 0)
+            host_gather(0, (1, 2, 3))
             nature(1, 1)
-        host_gather(1)
-        bits(0, 0)
-        bits(0, 1)
+        else:
+            host_gather(0, range(4))
+        host_gather(1, range(4))
+        for c in range(3):
+            bits(0, c)
         if first:
             join(1, 0, 0, 224)
             join(1, 0, 224, 448)
             bits(1, 0)
         tt(A("t2"), A("b2", by=A("hx", 0, 28)), A("ea" + k), ALU.mult)
-        bits(1, 1 if first else 0)
+        host_send(0)
         scan(A("s2"), A("t2"))
         if first:
-            host_send(0)
+            bits(1, 1)
+            bits(1, 2)
+            even(1)
+        else:
+            bits(1, 0)
+        tt(A("lf"), wrapped("s2"), wrapped("gw"), ALU.add)
+        if first:
+            join(1, 1, 0, 224)
         else:
             bits(1, 1)
-        copy(A("i2"), wrapped("s2"))
+        ts(A("l1"), A("lf"), 2 * BIG, ALU.add)
         if first:
-            join(1, 1, 0, 448)
+            join(1, 1, 224, 448)
+            host_send(1)
         else:
-            host_send(0)
-        ts(A("j2"), A("i2"), 1023, ALU.bitwise_and)
+            bits(1, 2)
         tt(A("t1"), A("b1", by=A("hx", 28, 56)), A("eb" + k), ALU.mult)
-        copy(A("l1"), A("j2"))
+        copy(A("wb", 448, 896), A("wb", 0, 448, by=A("l1")), "s")
         if first:
             nature(2, 0)
-            nature(2, 1)
-        copy(A("wb", 448, 896), A("wb", 0, 448, by=A("l1")), "s")
-        host_send(1)
+            gap()
+        else:
+            host_send(1)
         ts(A("n1"), A("t1"), 1023, ALU.bitwise_and)
-        scaled(A("x64"), A(xo), 64.0)
-        if first:
-            nature(3, 0)
-            nature(3, 1)
-        copy(A("l3", p=(0, 32)), A("j2", p=(0, 32)))
+        copy(A("l3", p=(0, 32)), A("l1", p=(0, 32)))
         gap()
         copy(A("wb", 896, 1344), A("n1", by=A("l1")))
         copy(A("l3", p=(0, 16)), A("idl", p=(0, 16)))
@@ -392,40 +397,49 @@ def rank_program(g, core, T, topo):
         ts(A("l2", p=(32, 64)), wrapped("s3", (0, 32)), BIG + 896.0, ALU.add)
         ts(A("l2", p=(96, 128)), wrapped("s3", (64, 96)), A("off", p=(64, 96)), ALU.add)
         ts(A("l3", p=(32, 64)), wrapped("s3", (0, 32)), A("off", p=(0, 32)), ALU.add)
-        gap()
-        copy(A("wb", 1344, 1792), A("wb", 0, 1344, by=A("l2")))
+        if s < 3:
+            gap()
+        halves("wb", 1344, 1344, "l2")
         gap()
         scan(A("s4"), A("wb", 1344, 1792))
         gap()
         ts(A("l3", p=(64, 96)), wrapped("s4", (32, 64)), A("off", p=(32, 64)), ALU.add)
         ts(A("l3", p=(96, 128)), wrapped("s4", (32, 64)), BIG + 1344.0, ALU.add)
         gap()
-        copy(A("o5"), A("wb", by=A("l3")))
+        halves("o5", 0, 1792, "l3")
+        if first:
+            nature(2, 1)
+            nature(3, 0)
+        elif s == 2:
+            nature(3, 1)
         gap()
         scan(A("s5"), A("o5"))
         gap()
         ts(A("vl" + k), wrapped("s5"), BIG, ALU.add)
         send(s, A("vr" + k), A("vl" + k), "k" + k)
         arrives(s, A("vr" + k), "k" + k)
-        if s == 3:
-            copy(A("o8"), A("n1", by=A("vl" + k)))
-            scan(A("s8"), A("o8"))
-            ts(A("l8"), wrapped("s8"), BIG, ALU.add)
-            send(s, A("r8"), A("l8"), "k8")
-            arrives(s, A("r8"), "k8")
-        if first:
-            quant(A("qe"), A("qes"), A("ec"))
-            quant(A("qv"), A("qvs"), A("vt"))
         gap(len(spare))
+        if s < 3:
+            even(s + 1)
         for c, (a, b) in enumerate(CHH):
             for t in range(4):
                 mm(bank(c, t, b - a), A("qe", 128 * t, 128 * t + 128), A("qes", 128 * t, 128 * t + 128), A("hc" + k, a, b), A("hcs" + k, a, b))
             for t in range(4):
                 tt(A("m" + k, 448 * t + a, 448 * t + b), A(xo, 4 * a + t, 4 * b, 4), bank(c, t, b - a), ALU.max)
+            if s == 3 and c == 0:
+                copy(A("o8"), A("n1", by=A("vl" + k)))
+        if s == 3:
+            scan(A("s8"), A("o8"))
+            quant(A("qv"), A("qvs"), A("vt"))
+            ts(A("l8"), wrapped("s8"), BIG, ALU.add)
+            send(s, A("r8"), A("l8"), "k8")
+            arrives(s, A("r8"), "k8")
+        else:
+            join(s + 1, 1, 0, 224)
 
-        def mosaic(c, t):
+        def mosaic(c, t, q):
             a, b = CHZ[c]
-            copy(A("z" + k, 4 * a + t, 4 * b, 4), A("m" + k, 448 * t, 448 * t + 448, by=A("vr" + k, a // 16, b // 16)), "v" if t < 2 else "s")
+            copy(A("z" + k, 4 * a + t, 4 * b, 4), A("m" + k, 448 * t, 448 * t + 448, by=A("vr" + k, a // 16, b // 16)), q)
 
         def layer(c):
             a, b = CHZ[c]
@@ -441,35 +455,35 @@ def rank_program(g, core, T, topo):
                 scaled(A(xn, 4 * a + t, 4 * b, 4), A("tmp", 448 * t + a, 448 * t + b), 2.0 ** -6)
 
         for c in range(3):
-            mosaic(c, 2)
-            mosaic(c, 3)
+            mosaic(c, 2, "s")
+            mosaic(c, 3, "s")
+        mosaic(2, 1, "s")
         if s == 3:
             copy(A("p7"), A("wb", 0, 448, by=A("vr3")), "s")
             dma("y", ext(T.pl[0:7, :]), (T.p7[16:128:16, :], A("p7")[1]), "op_")
-        mosaic(0, 0)
-        mosaic(0, 1)
-        mosaic(1, 0)
+        mosaic(0, 0, "v")
+        mosaic(0, 1, "v")
+        mosaic(1, 0, "v")
         layer(0)
-        mosaic(1, 1)
-        mosaic(2, 0)
+        mosaic(1, 1, "v")
+        mosaic(2, 0, "v")
         layer(1)
-        mosaic(2, 1)
         finish(0)
         layer(2)
         finish(1)
         finish(2)
+        for c in range(3):
+            settle(s, c)
+        if s < 3:
+            join(s + 1, 1, 224, 448)
 
-    for c, (a, b) in enumerate(CHX):
-        quant(A("qx3", a, b), A("qxs3", a, b), A("x3", 4 * a, 4 * b))
-        mm(A("pa", 512 * c, 512 * c + b - a), A("qv"), A("qvs"), A("qx3", a, b), A("qxs3", a, b))
-        dma("y", ext(T.oc[:, 4 * a:4 * b]), A("qx3", a, b, cast=dt.uint8), "oo")
-    copy(A("p8"), A("wb", 0, 448, by=A("r8")), "s")
     for i in range(4):
-        dma("s", ext(T.osc[4 * i:4 * i + 4, :]), A("qxs3", p=(32 * i, 32 * i + 4)), "os_")
+        dma("y", ext(T.osc[4 * i:4 * i + 4, :]), A("qxs3", p=(32 * i, 32 * i + 4)), "os_")
+    for c, (a, b) in enumerate(CHZ):
+        copy(A("yb", a, b), score(c, b - a), "ssv"[c])
+    dma("y", ext(T.y[:, :]), A("yb"), "oy")
+    copy(A("p8"), A("wb", 0, 448, by=A("r8")), "s")
     dma("s", ext(T.pl[7:8, :]), A("p8", p=(112, 113)), "op_")
-    for c, (a, b) in enumerate(CHX):
-        copy(A("yb", a, b), A("pa", 512 * c, 512 * c + b - a))
-        dma("y", ext(T.y[:, a:b]), A("yb", a, b), "oy")
     for sem in sorted(total):
         if seen["p"].get(sem, 0) < total[sem]:
             g.wait_ge(T.sem[sem], total[sem])

from concourse.bass import DstId, RemoteDMATransfer
from concourse.mybir import dt, AluOpType, ActivationFunctionType

C = 448
STEPS = (1, 2, 3)
CHH = ((0, 224), (224, 448))
CHZ = ((0, 160), (160, 320), (320, 448))
CHL = ((0, 320), (320, 448))
PIECE = 112
BIG = 524288.0
ALU = AluOpType
COPY = ActivationFunctionType.Copy
F8, U8, BF, F32, I32, U16 = "float8_e4m3fn_x4", "uint8", "bfloat16", "float32", "int32", "uint16"

SCRATCH = {"pa": ("psum", [128, 2048], F32), "pb": ("psum", [128, 2048], F32)}


def _sbuf(kind, **widths):
    for name in widths:
        SCRATCH[name] = ("sbuf", [128, widths[name]], kind)


_sbuf(I32, gli=56, hti=28, uli=16, pi=1, lo=1, hi=1, idl=28, t1=448, n1=448)
_sbuf(U16, gs=112, hx=56, hl=112, ul=16, l1=28, l2=28, l3=28, l8=28, r8=28)
_sbuf(BF, ut=512, vt=512, ec=2048, eye=128, x64=1792)
_sbuf(F8, qu=128, qp=256, qv=128, qe=512, qw=512)
_sbuf(U8, qus=128, qps=256, qvs=128, qes=512, qws=512)
_sbuf(F32, wt=96, tg=128, tg2=128, th=64, th2=64, lof=1, off=1, m16=16, da=16, db=16, dc=16, dd=16, de=16, d=448, gw=448,
      wb=1792, b1=448, b2=448, t2=448, s2=448, s3=448, s4=448, o5=448, s5=448, lf=28, na0=896, nb0=896, na1=896, nb1=896,
      tmp=1792, o8=448, s8=448, p7=448, p8=448, yb=448)
for _k in range(4):
    SCRATCH["x%d" % _k] = ("sbuf", [128, 1792], BF)
    SCRATCH["qx%d" % _k] = ("sbuf", [128, 448], F8)
    SCRATCH["qxs%d" % _k] = ("sbuf", [128, 448], U8)
for _k in STEPS:
    for _n, _w, _d in (("h", 1792, BF), ("m", 1792, BF), ("z", 1792, BF), ("qh", 448, F8), ("hc", 448, F8), ("qz", 448, F8),
                       ("qhs", 448, U8), ("hcs", 448, U8), ("qzs", 448, U8), ("vl", 28, U16), ("vr", 28, U16), ("gr", 112, U16),
                       ("ea", 448, F32), ("eb", 448, F32)):
        SCRATCH["%s%d" % (_n, _k)] = ("sbuf", [128, _w], _d)
SEMAPHORES = ["v", "s", "t", "p", "rl", "k8", "dgl", "dht", "dx0", "dx1", "du", "dw", "dv", "oo", "os_", "oy", "op_"]
for _k in STEPS:
    SEMAPHORES += ["g%d" % _k, "k%d" % _k, "c%da" % _k, "c%db" % _k]


def rank_program(g, core, T, topo):
    rank = T.rank_of(core)
    if rank is None:
        return
    queue = {"v": g.vector, "s": g.scalar, "t": g.tensor, "p": g, "y": g.sync}
    total, log = {}, {}
    seen = dict((q, {}) for q in queue)

    def A(name, a=0, b=None, step=1, p=None, cast=None, by=None):
        t = T[name]
        b = t.shape[1] if b is None else b
        lo, hi = p if p else (0, 128)
        reg = [(name, lo, hi, a, b, step)]
        if name in ("pa", "pb"):
            reg = [(name, 0, 128, a // 512 * 512, (b + 511) // 512 * 512, 1)]
        if p:
            v = t[lo:hi, a:b:step] if step > 1 else t[lo:hi, a:b]
        else:
            v = t[:, a:b:step] if step > 1 else t[:, a:b]
        if cast is not None:
            v = v.bitcast(cast)
        if by is not None:
            v = v.indirect(by[0])
            reg = reg + by[1]
        return v, reg

    def touch(r, s):
        apart = r[5] == s[5] and (r[3] - s[3]) % r[5] != 0
        return r[1] < s[2] and s[1] < r[2] and r[3] < s[4] and s[3] < r[4] and not apart

    def covers(r, s):
        same = r[5] == 1 or r[5] == s[5] and (r[3] - s[3]) % r[5] == 0
        return r[1] <= s[1] and s[2] <= r[2] and r[3] <= s[3] and s[4] <= r[4] and same

    def waits(q, reads, writes):
        need = {}
        for regs, wr in ((reads, False), (writes, True)):
            for r in regs:
                for reg, was, sem, val in log.get(r[0], []):
                    if touch(r, reg) and (wr or was or r[0] in ("pa", "pb")):
                        need[sem] = max(need.get(sem, 0), total[sem] if val is None else val)
        for sem in sorted(need):
            if seen[q].get(sem, 0) < need[sem]:
                queue[q].wait_ge(T.sem[sem], need[sem])
                seen[q][sem] = need[sem]

    def note(reads, writes, sem, val):
        for r in writes:
            log[r[0]] = [e for e in log.get(r[0], []) if not covers(r, e[0])] + [(r, True, sem, val)]
        for r in reads:
            log.setdefault(r[0], []).append((r, False, sem, val))

    def run(q, call, outs, ins):
        reads = [r for o in ins for r in o[1]]
        writes = [r for o in outs for r in o[1]]
        waits(q, reads, writes)
        call().then_inc(T.sem[q], 1)
        total[q] = total.get(q, 0) + 1
        note(reads, writes, q, total[q])

    def dma(q, out, in_, sem):
        waits(q, in_[1], out[1])
        queue[q].dma_start(out[0], in_[0]).then_inc(T.sem[sem], 16)
        total[sem] = total.get(sem, 0) + 16
        note(in_[1], out[1], sem, None)

    def ext(view):
        return view, []

    def core_of(step):
        return T.cores[rank ^ step]

    def send(step, out, in_, sem):
        dst = core_of(step)
        waits("p", in_[1], [])
        rid, pid, _ = topo.addr(dst)
        g.remote_dma(out[0], in_[0], T.sem[sem], T.sem.rl, pid, rid, topo.mask(core, dst))
        total["rl"] = total.get("rl", 0) + len(topo.engines(core, dst))

    def send_both():
        mv = []
        waits("p", A("gs")[1], [])
        for j, st in enumerate((2, 3)):
            dst = core_of(st)
            rid, pid, _ = topo.addr(dst)
            eng = topo.engines(core, dst)
            mine = eng[len(eng) // 2 * j:len(eng) // 2 * (j + 1)]
            mv.append(RemoteDMATransfer(dst_ids=[DstId(rid=rid, pnc=pid)], dma_engine_mask=sum(1 << e for e in mine),
                                        remote_sem=T.sem["g%d" % st], src=T.gs[:, :], dst=T["gr%d" % st][:, :]))
            total["rl"] = total.get("rl", 0) + len(mine)
        g.remote_dma_fused(mv, local_sem=T.sem.rl)

    def arrives(step, out, sem, part=1):
        total[sem] = total.get(sem, 0) + len(topo.engines(core_of(step), core)) // part
        note([], out[1], sem, None)

    def copy(out, in_, q="v"):
        if q == "v":
            run("v", lambda: g.vector.tensor_copy(out[0], in_[0]), [out], [in_])
        else:
            run("s", lambda: g.scalar.activation(out[0], in_[0], COPY), [out], [in_])

    def scaled(out, in_, c):
        run("s", lambda: g.scalar.activation(out[0], in_[0], COPY, scale=c), [out], [in_])

    def ts(out, in_, a, op0, b=None, op1=None):
        col = [a] if isinstance(a, tuple) else []
        a0 = a[0] if col else a
        if op1 is None:
            run("v", lambda: g.vector.tensor_scalar(out[0], in_[0], a0, None, op0), [out], [in_] + col)
        else:
            run("v", lambda: g.vector.tensor_scalar(out[0], in_[0], a0, b, op0, op1), [out], [in_] + col)

    def tt(out, a, b, op):
        run("v", lambda: g.vector.tensor_tensor(out[0], a[0], b[0], op), [out], [a, b])

    def fill(out, c):
        run("v", lambda: g.vector.memset(out[0], c), [out], [])

    def turn(out, in_):
        run("v", lambda: g.vector.transpose(out[0], in_[0]), [out], [in_])

    def quant(q, s, in_):
        run("v", lambda: g.vector.quantize_mx(q[0], s[0], in_[0]), [q, s], [in_])

    def mm(out, l, ls, r, rs):
        run("t", lambda: g.tensor.matmul_mx(out[0], l[0], ls[0], r[0], rs[0], True, True), [out], [l, ls, r, rs])

    def iota(out, pattern, base, cm, f=False):
        if f:
            run("p", lambda: g.iota(out[0], pattern, base, cm, allow_small_or_imprecise_dtypes=True), [out], [])
        else:
            run("p", lambda: g.iota(out[0], pattern, base, cm), [out], [])

    def scan(out, in_):
        d = A("d")
        run("v", lambda: g.vector.tensor_tensor_scan(out[0], in_[0], d[0], -BIG, ALU.max, ALU.add), [out], [in_, d])

    def wrapped(name, p=None):
        return A(name, 15, 448, 16, p)

    def bank(c, t, n):
        return A(("pa", "pb")[c % 2], 512 * t, 512 * t + n)

    def score(i, n):
        return A(("pb", "pa")[i // 4], 512 * (i % 4), 512 * (i % 4) + n)

    spare = []

    def gap(n=1):
        while n and spare:
            spare.pop(0)()
            n -= 1

    dma("y", A("gli"), ext(T.gl[:, :]), "dgl")
    dma("s", A("hti"), ext(T.ht[:, :]), "dht")
    for k, (a, b) in enumerate(CHL):
        dma("s" if k == 0 else "y", A("x0", 4 * a, 4 * b), ext(T.x[:, 4 * a:4 * b]), "dx%d" % k)
    dma("y", A("ut"), ext(T.u[:, :]), "du")
    waits("y", A("x0")[1] + A("ut")[1], [])
    dma("y", A("qws"), ext(T.ws[:, :]), "dw")
    dma("y", A("qw", cast=dt.uint8), ext(T.wc[:, :]), "dw")
    dma("y", A("vt"), ext(T.v[:, :]), "dv")

    for k in range(4):
        spare.append(lambda k=k: fill(A("ec", 512 * k, 512 * k + 512), 0.0))
    fill(A("eye"), 1.0)
    iota(A("m16"), [[1, 16]], 0, 0, True)
    iota(A("pi"), [[0, 1]], 0, 1)
    iota(A("uli"), [[16, 2], [32, 4], [0, 2]], 0, 0)
    run("p", lambda: g.affine_select(T.eye[:, :], T.eye[:, :], [[-1, 128]], ALU.is_equal, 0.0, 0, 1), [A("eye")], [A("eye")])
    iota(A("idl"), [[16, 28]], 0, 1)
    iota(A("wb", 0, 448), [[1, 448]], 0, 0, True)
    fill(A("wt"), 0.0)
    fill(A("l2"), 0)
    gap(2)
    ts(A("lo"), A("pi"), 15, ALU.bitwise_and)
    ts(A("hi"), A("pi"), 4, ALU.logical_shift_right, 1, ALU.bitwise_and)
    ts(A("dc"), A("m16"), 15.0, ALU.is_equal, -2.0, ALU.mult)
    copy(A("ul"), A("uli"))
    copy(A("lof"), A("lo"))
    ts(A("off"), A("hi"), 448.0, ALU.mult, BIG, ALU.add)
    gap()
    ts(A("da"), A("m16"), A("lof"), ALU.is_ge)
    ts(A("db"), A("m16"), A("lof"), ALU.is_equal)
    gap()
    tt(A("dd"), A("da"), A("db"), ALU.add)
    for t in range(4):
        copy(A("ec", 513 * t, 512 * t + 512, 4), A("eye"), "s")
    copy(A("wt", 0, 56), A("gli"))
    tt(A("de"), A("dd"), A("dc"), ALU.add)
    turn(A("tg", 0, 64), A("wt", 0, 64))
    turn(A("tg", 64, 128), A("wt", 0, 64))
    ts(A("d", 0, 16), A("de"), -1.0, ALU.add, BIG, ALU.mult)
    w = [16]

    def widen():
        if w[0] < C:
            n = min(w[0], C - w[0])
            copy(A("d", w[0], w[0] + n), A("d", 0, n))
            w[0] += n

    for k in (0, 32):
        copy(A("tg", k + 16, k + 32), A("tg", k, k + 16))
        copy(A("tg", 64 + k, 64 + k + 16), A("tg", 64 + k + 16, 64 + k + 32))
    widen()
    turn(A("tg2"), A("tg"))
    widen()
    copy(A("gs", 0, 56), A("tg2", 0, 56))
    copy(A("gs", 56, 112), A("tg2", 64, 120))
    send(1, A("gr1"), A("gs"), "g1")
    send_both()
    for s in STEPS:
        arrives(s, A("gr%d" % s), "g%d" % s, 1 if s == 1 else 2)
    copy(A("wt", 64, 92), A("hti"))
    for t in range(4):
        ts(A("hl", 28 * t, 28 * t + 28), A("hti"), 4.0, ALU.mult, float(t), ALU.add)
    turn(A("th", 0, 32), A("wt", 64, 96))
    turn(A("th", 32, 64), A("wt", 64, 96))
    widen()
    widen()
    copy(A("th", 16, 32), A("th", 0, 16))
    copy(A("th", 32, 48), A("th", 48, 64))
    widen()
    turn(A("th2"), A("th"))
    quant(A("qe"), A("qes"), A("ec"))
    copy(A("hx", 0, 28), A("th2", 0, 28))
    copy(A("hx", 28, 56), A("th2", 32, 60))
    quant(A("qu"), A("qus"), A("ut"))
    ul = A("ul")
    copy(A("qps"), A("qus", by=ul), "s")
    copy(A("qp", cast=dt.uint32), A("qu", cast=dt.uint32, by=ul))

    def nature(s, wave):
        nat = ("na%d", "nb%d")[wave] % (s % 2)
        lst = 56 * wave
        if s == 1 and wave == 0:
            copy(A(nat, 0, 448), A("wb", 0, 448, by=A("gr1", 0, 28)))
            copy(A(nat, 448, 896), A("wb", 0, 448, by=A("gr1", 28, 56)), "s")
        else:
            copy(A(nat), A("wb", 0, 448, by=A("gr%d" % s, lst, lst + 56)), "s")
        if wave:
            scaled(A(nat, 0, 896, 2), A(nat, 0, 896, 2), 1024.0)

    def join(s, wave, a, b):
        nat = ("na%d", "nb%d")[wave] % (s % 2)
        tt(A(("ea%d", "eb%d")[wave] % s, a, b), A(nat, 2 * a + 1, 2 * b, 2), A(nat, 2 * a, 2 * b, 2), (ALU.subtract, ALU.add)[wave])

    def even(s):
        scan(A("gw"), A("na%d" % (s % 2), 0, 896, 2))

    def halves(out, a, b, name):
        copy(A(out, a, a + 224), A("wb", 0, b, by=A(name, 0, 14)))
        copy(A(out, a + 224, a + 448), A("wb", 0, b, by=A(name, 14, 28)), "s")

    def settle(s, c):
        a, b = CHZ[c]
        q, sc = A("qx%d" % s, a, b), A("qxs%d" % s, a, b)
        quant(q, sc, A("x%d" % s, 4 * a, 4 * b))
        if s < 3:
            mm(score(c, b - a), A("qp", 0, 128), A("qps", 0, 128), q, sc)
        else:
            mm(score(c, b - a), A("qv"), A("qvs"), q, sc)
            if c:
                a, b = CHL[c - 1]
                dma("y", ext(T.oc[:, 4 * a:4 * b]), A("qx3", a, b, cast=dt.uint8), "oo")

    for c in range(3):
        settle(0, c)
    for s in STEPS:
        k = "%d" % s
        xo, xn = "x%d" % (s - 1), "x" + k
        qx, qxs = "qx%d" % (s - 1), "qxs%d" % (s - 1)
        first = s == 1
        for a in range(0, 1792, 448):
            spare.append(lambda a=a: ts(A("x64", a, a + 448), A(xo, a, a + 448), 64.0, ALU.mult))
        if s < 3:
            for a in range(0, C, PIECE):
                spare.append(lambda a=a: join(s + 1, 0, a, a + PIECE))

        def host_gather(c, which):
            a, b = CHH[c]
            for t in which:
                copy(A("h" + k, 4 * a + t, 4 * b, 4), A(xo, by=A("hl", 28 * t + a // 16, 28 * t + b // 16)), "s")

        def host_send(c):
            a, b = CHH[c]
            quant(A("qh" + k, a, b), A("qhs" + k, a, b), A("h" + k, 4 * a, 4 * b))
            sem = "c" + k + "ab"[c]
            send(s, A("hc" + k, a, b, cast=dt.uint8), A("qh" + k, a, b, cast=dt.uint8), sem)
            send(s, A("hcs" + k, a, b), A("qhs" + k, a, b), sem)
            arrives(s, A("hc" + k, a, b), sem)
            arrives(s, A("hcs" + k, a, b), sem)

        def bits(n, c):
            a, b = CHZ[c]
            if n == 0:
                ts(A("b2", a, b), score(c, b - a), 0.0, ALU.is_gt)
            else:
                ts(A("b1", a, b), score(3 + c, b - a), 0.0, ALU.is_gt, 2.0 ** -10, ALU.max)

        for c, (a, b) in enumerate(CHZ):
            mm(score(3 + c, b - a), A("qp", 128, 256), A("qps", 128, 256), A(qx, a, b), A(qxs, a, b))
        if first:
            host_gather(0, (0,))
            nature(1, 0)
            host_gather(0, (1, 2, 3))
            nature(1, 1)
        else:
            host_gather(0, range(4))
        host_gather(1, range(4))
        for c in range(3):
            bits(0, c)
        if first:
            join(1, 0, 0, 224)
            join(1, 0, 224, 448)
            bits(1, 0)
        tt(A("t2"), A("b2", by=A("hx", 0, 28)), A("ea" + k), ALU.mult)
        host_send(0)
        scan(A("s2"), A("t2"))
        if first:
            bits(1, 1)
            bits(1, 2)
            even(1)
        else:
            bits(1, 0)
        tt(A("lf"), wrapped("s2"), wrapped("gw"), ALU.add)
        if first:
            join(1, 1, 0, 224)
        else:
            bits(1, 1)
        ts(A("l1"), A("lf"), 2 * BIG, ALU.add)
        if first:
            join(1, 1, 224, 448)
            host_send(1)
        else:
            bits(1, 2)
        tt(A("t1"), A("b1", by=A("hx", 28, 56)), A("eb" + k), ALU.mult)
        copy(A("wb", 448, 896), A("wb", 0, 448, by=A("l1")), "s")
        if first:
            nature(2, 0)
            gap()
        else:
            host_send(1)
        ts(A("n1"), A("t1"), 1023, ALU.bitwise_and)
        copy(A("l3", p=(0, 32)), A("l1", p=(0, 32)))
        gap()
        copy(A("wb", 896, 1344), A("n1", by=A("l1")))
        copy(A("l3", p=(0, 16)), A("idl", p=(0, 16)))
        gap()
        scan(A("s3"), A("wb", 896, 1344))
        gap()
        ts(A("l2", p=(32, 64)), wrapped("s3", (0, 32)), BIG + 896.0, ALU.add)
        ts(A("l2", p=(96, 128)), wrapped("s3", (64, 96)), A("off", p=(64, 96)), ALU.add)
        ts(A("l3", p=(32, 64)), wrapped("s3", (0, 32)), A("off", p=(0, 32)), ALU.add)
        if s < 3:
            gap()
        halves("wb", 1344, 1344, "l2")
        gap()
        scan(A("s4"), A("wb", 1344, 1792))
        gap()
        ts(A("l3", p=(64, 96)), wrapped("s4", (32, 64)), A("off", p=(32, 64)), ALU.add)
        ts(A("l3", p=(96, 128)), wrapped("s4", (32, 64)), BIG + 1344.0, ALU.add)
        gap()
        halves("o5", 0, 1792, "l3")
        if first:
            nature(2, 1)
            nature(3, 0)
        elif s == 2:
            nature(3, 1)
        gap()
        scan(A("s5"), A("o5"))
        gap()
        ts(A("vl" + k), wrapped("s5"), BIG, ALU.add)
        send(s, A("vr" + k), A("vl" + k), "k" + k)
        arrives(s, A("vr" + k), "k" + k)
        gap(len(spare))
        if s < 3:
            even(s + 1)
        for c, (a, b) in enumerate(CHH):
            for t in range(4):
                mm(bank(c, t, b - a), A("qe", 128 * t, 128 * t + 128), A("qes", 128 * t, 128 * t + 128), A("hc" + k, a, b), A("hcs" + k, a, b))
            for t in range(4):
                tt(A("m" + k, 448 * t + a, 448 * t + b), A(xo, 4 * a + t, 4 * b, 4), bank(c, t, b - a), ALU.max)
            if s == 3 and c == 0:
                copy(A("o8"), A("n1", by=A("vl" + k)))
        if s == 3:
            scan(A("s8"), A("o8"))
            quant(A("qv"), A("qvs"), A("vt"))
            ts(A("l8"), wrapped("s8"), BIG, ALU.add)
            send(s, A("r8"), A("l8"), "k8")
            arrives(s, A("r8"), "k8")
        else:
            join(s + 1, 1, 0, 224)

        def mosaic(c, t, q):
            a, b = CHZ[c]
            copy(A("z" + k, 4 * a + t, 4 * b, 4), A("m" + k, 448 * t, 448 * t + 448, by=A("vr" + k, a // 16, b // 16)), q)

        def layer(c):
            a, b = CHZ[c]
            quant(A("qz" + k, a, b), A("qzs" + k, a, b), A("z" + k, 4 * a, 4 * b))
            for t in range(4):
                mm(bank(c, t, b - a), A("qw", 128 * t, 128 * t + 128), A("qws", 128 * t, 128 * t + 128),
                   A("qz" + k, a, b), A("qzs" + k, a, b))

        def finish(c):
            a, b = CHZ[c]
            for t in range(4):
                tt(A("tmp", 448 * t + a, 448 * t + b), bank(c, t, b - a), A("x64", 4 * a + t, 4 * b, 4), ALU.add)
                scaled(A(xn, 4 * a + t, 4 * b, 4), A("tmp", 448 * t + a, 448 * t + b), 2.0 ** -6)

        for c in range(3):
            mosaic(c, 2, "s")
            mosaic(c, 3, "s")
        mosaic(2, 1, "s")
        if s == 3:
            copy(A("p7"), A("wb", 0, 448, by=A("vr3")), "s")
            dma("y", ext(T.pl[0:7, :]), (T.p7[16:128:16, :], A("p7")[1]), "op_")
        mosaic(0, 0, "v")
        mosaic(0, 1, "v")
        mosaic(1, 0, "v")
        layer(0)
        mosaic(1, 1, "v")
        mosaic(2, 0, "v")
        layer(1)
        finish(0)
        layer(2)
        finish(1)
        finish(2)
        for c in range(3):
            settle(s, c)
        if s < 3:
            join(s + 1, 1, 224, 448)

    for i in range(4):
        dma("y", ext(T.osc[4 * i:4 * i + 4, :]), A("qxs3", p=(32 * i, 32 * i + 4)), "os_")
    for c, (a, b) in enumerate(CHZ):
        copy(A("yb", a, b), score(c, b - a), "ssv"[c])
    dma("y", ext(T.y[:, :]), A("yb"), "oy")
    copy(A("p8"), A("wb", 0, 448, by=A("r8")), "s")
    dma("s", ext(T.pl[7:8, :]), A("p8", p=(112, 113)), "op_")
    for sem in sorted(total):
        if seen["p"].get(sem, 0) < total[sem]:
            g.wait_ge(T.sem[sem], total[sem])
